import numpy as np, ml_dtypes
CORES = [48,51,52,55]
N = 4
BF = ml_dtypes.bfloat16
C, V, VX, STEPS = 256, 2048, 4096, 5
def parts(rng):
    x = rng.integers(0, 32, (N, 8, 16, VX), dtype=np.int32); rb = rng.integers(0, V, (N, 8, 16, V), dtype=np.int32)
    a = rng.integers(0, V, (N, 8, 16, C), dtype=np.int32); h = rng.integers(0, 32, (N, 8, 16, C), dtype=np.int32)
    th = rng.integers(80, 135, (N, 8, 16, 1)) + rng.integers(-12, 13, (N, 8, 1, 1)); w = rng.integers(0, 256, (N, 8, 16, 1))
    return x, rb, a, h, th, w
def pack(x, rb, a, h, th, w):
    return {"cues": x.reshape(N, 128, VX).astype(np.float32).astype(BF), "spare": rb.reshape(N, 128, V).astype(np.int32), "scroll": a.reshape(N, 128, C).astype(np.int32),
            "heard": h.reshape(N, 128, C).astype(np.float32).astype(BF), "th": th.reshape(N, 128, 1).astype(np.int32), "w": w.reshape(N, 128, 1).astype(np.int32)}
def setup_inputs(rng):
    return pack(*parts(rng))
def setup_inputs_corners(rng):
    x, rb, a, h, th, w = parts(rng); lane = np.arange(16).reshape(1, 1, 16, 1); n = np.arange(V); c = np.arange(C)
    u = rng.random((N, 8, 1, VX)); x = np.where(u < 0.1, 0, np.where(u < 0.2, 31, x)); u = rng.random((N, 8, 1, C)); h = np.where(u < 0.1, 0, np.where(u < 0.2, 31, h))
    rb = np.choose(rng.integers(0, 5, rb.shape), [0, V - 1, n, (n + 1) % V, rb]); a = np.choose(rng.integers(0, 5, a.shape), [0, V - 1, c, V - C + c, a])
    kd = np.argsort(rng.random((N, 8)), axis=1).reshape(N, 8, 1, 1); j = rng.integers(0, 16, (N, 8, 1, 1)); mid = rng.integers(80, 135, (N, 8, 16, 1))
    th = np.choose(kd, [496, 496 * (lane == 15), 0, 496 * (lane == j), mid, 496 * (lane % 2), mid, mid]); w = np.where(kd == 6, 255, np.where(kd == 7, 0, w))
    q = rng.permutation(N); th[q[0]] = 496; th[q[1]] = 0
    return pack(x, rb, a, h, th, w)
def setup_inputs_ends(rng):
    def two(hi, *shape): return np.where(rng.random(shape) < 0.5, hi, 0)
    lane = np.arange(16).reshape(1, 1, 16, 1)
    u = rng.random((N, 8, 1, VX)); u[..., 1] = 1.0; u[..., V - 2] = 1.0; x = np.where(u < 0.3, 0, np.where(u < 0.6, 31, two(31, N, 8, 16, VX)))
    u = rng.random((N, 8, 1, C)); h = np.where(u < 0.25, 0, np.where(u < 0.5, 31, two(31, N, 8, 16, C)))
    rb = two(V - 1, N, 8, 16, V); u = rng.random((N, 8, 1, V)); rb = np.where(u < 0.1, 0, np.where(u < 0.2, V - 1, rb)); a = two(V - 1, N, 8, 16, C)
    w = two(255, N, 8, 16, 1); w[:, 0, 0] = 0; w[:, 0, 1] = 255; w[:, 7] = 255
    j = rng.integers(0, 16, (N, 8, 1, 1)); only = rng.random((N, 8, 1, 1)) < 0.3; none = rng.random((N, 8, 1, 1)) < 0.4; none[0] = False; none[:, 0] = False; none[N - 1, 7] = True
    th = np.where(lane == j, 496, two(496, N, 8, 16, 1)); th = np.where(only, 496 * (lane == 15), th); th = np.where(none, 0, th); th[:, 0, 0] = 0; th[:, 0, 15] = 496
    s = (16 * 255 * 31) & (VX - 1); x[:, 7, :, s] = 0; x[:, 7, :, (s + V - 1) & (VX - 1)] = 0; x[:, 7, :, V - 2] = 31
    m = rng.random((N, 1, C)) < 0.2; m[..., [0, 1, C - 2, C - 1]] = True; h[:, 7] = np.where(m, 31, h[:, 7])
    return pack(x, rb, a, h, th, w)
def setup_inputs_far(rng):
    x, rb, a, h, th, w = parts(rng); x = rng.integers(20, 32, x.shape); h = rng.integers(0, 4, h.shape)
    half = np.argsort(rng.random((N, 8)), axis=1).reshape(N, 8, 1, 1) & 1
    th = np.where(half == 1, rng.integers(345, 396, (N, 8, 16, 1)), 0)
    q = int(rng.integers(0, N)); p = (q + 1) % N; b = (q - 1) % N; g0 = int(rng.integers(0, 8)); rest = [g for g in range(8) if g != g0]
    x[b] = rng.integers(0, 4, x[b].shape)
    for r, count in ((q, 3 * C + int(rng.integers(8, 16))), (p, 7 * C)):
        th[r] = rng.integers(40, 65, (8, 16, 1)); hit = np.zeros(7 * C, bool); hit[rng.permutation(7 * C)[:count]] = True; hit = hit.reshape(7, C)
        for i, g in enumerate(rest):
            to = (np.arange(VX) - np.add.reduce(w[r, g] * x[r, g], axis=0)) & (VX - 1); can = np.nonzero(to < V)[0]
            c = np.nonzero(hit[i])[0]; n = can[rng.integers(0, len(can), len(c))]
            h[r, g][:, c] = x[r, g][:, n]; a[r, g, rng.integers(0, 16, len(c)), c] = to[n]
    e = rng.integers(-1, 2, (N, 8, C)); h[:, g0, 0::2] = 30 + e; h[:, g0, 1::2] = 30 - e
    x[:, g0, :, :V] = 31; x[:, g0, :, V:] = 0; w[:, g0] = V // 16
    th[:, g0] = rng.choice(np.array([0, 15, 16, 479, 480]), (N, 16, 1)); th[np.arange(N), g0, rng.integers(0, 15, N)] = 480
    return pack(x, rb, a, h, th, w)
def setup_inputs_spread(rng):
    x, rb, a, h, th, w = parts(rng)
    x = np.minimum((np.exp2(5 * rng.random((N, 8, 1, VX))) * rng.random(x.shape) + 0.5).astype(np.int64), 31); h = np.minimum((np.exp2(5 * rng.random((N, 8, 1, C))) * rng.random(h.shape) + 0.5).astype(np.int64), 31)
    def uneven(top, shape, flip):
        v = np.minimum(np.power(float(top), rng.random(shape)).astype(np.int64), top) - 1
        return np.where(rng.random(flip) < 0.3, top - 1 - v, v)
    rb = uneven(V, rb.shape, (N, 8, 1, V)); a = uneven(V, a.shape, (N, 8, 1, C)); w = uneven(256, w.shape, (N, 8, 1, 1))
    th = np.minimum(uneven(497, th.shape, (N, 8, 16, 1)), rng.choice(np.array([20, 60, 110, 496]), (N, 8, 1, 1)))
    return pack(x, rb, a, h, th, w)
def setup_inputs_ties(rng):
    x, rb, a, h, th, w = parts(rng)
    o = rng.integers(6, 26, (N, 8, 16, 2)); e = rng.integers(-6, 7, (N, 8, 16)); pool = rng.integers(0, 32, (N, 8, 16, 4)); pool[..., 0] = o[..., 0] + e; pool[..., 1] = o[..., 0] - e
    x = np.take_along_axis(pool, rng.integers(0, 4, (N, 8, 1, VX)), 3); h = np.take_along_axis(o, (rng.random((N, 8, 1, C)) < 0.3).astype(np.int64), 3)
    less = np.stack([rng.permutation(8) % 2 for q in range(N)])
    th = np.broadcast_to(np.maximum(np.add.reduce(np.abs(e), axis=2) - less, 0)[:, :, None, None], (N, 8, 16, 1))
    a = np.where(rng.random((N, 8, 1, C)) < 0.25, a[:, :, 3:4], a)
    return pack(x, rb, a, h, th, w)
def check_inputs(d):
    bad = []
    for k, hi in (("cues", 31), ("spare", V - 1), ("scroll", V - 1), ("heard", 31), ("th", 496), ("w", 255)):
        v = np.asarray(d[k]).astype(np.float64)
        if not (np.all(v >= 0) and np.all(v <= hi)): bad.append("range of " + k)
        elif np.any(v != np.floor(v)): bad.append("whole numbers in " + k)
    return bad
def reference(cues, spare, scroll, heard, th, w):
    x = cues.astype(np.float32).astype(np.int32).reshape(N, 8, 16, VX); rb = spare.astype(np.int32).reshape(N, 8, 16, V); gb = np.array(rb)
    a = scroll.astype(np.int32).reshape(N, 8, 16, C); h = heard.astype(np.float32).astype(np.int32).reshape(N, 8, 16, C)
    limit = th.astype(np.int32).reshape(N, 8, 16, 1); weight = w.astype(np.int32).reshape(N, 8, 16, 1)
    head = np.zeros((N, 8, C), np.int32); wait = np.zeros((N, 8, C), np.int32); m = [0] * N; place = np.arange(16, dtype=np.int32)[None, :, None]
    for t in range(STEPS):
        say = []
        for r in range(N):
            old = a[r]; hr = h[r]
            shift = np.add.reduce(weight[r] * hr, axis=1) & (VX - 1)
            at = (old + shift[:, None, :]) & (VX - 1)
            px = np.take_along_axis(x[r], at.reshape(8, 1, 16 * C), 2).reshape(8, 16, 16, C)
            d = np.add.reduce(np.abs(px - hr[:, :, None, :]), axis=1)
            o = (place - head[r][:, None, :]) & 15
            near = d <= limit[r] + (m[r] & 15); got = np.any(near, axis=1)
            k = np.argmin(np.where(near, o, 16 + 16 * d + o), axis=1)
            upto = (k - head[r]) & 15
            ak = np.take_along_axis(old, k[:, None, :], 1)[:, 0]
            xk = np.take_along_axis(px, k[:, None, None, :], 2)[:, :, 0]
            rk = np.take_along_axis(rb[r], ak[:, None, :], 2); gk = np.take_along_axis(gb[r], ak[:, None, :], 2)
            sk = np.take_along_axis(x[r], (ak ^ 1)[:, None, :], 2)
            say.append(np.where(got[:, None, :], sk, np.abs(hr - xk)))
            more = np.where(got, 0, wait[r] + 1); full = more == 2
            new = np.where(got[:, None, :] & (o <= upto[:, None, :]), rk, np.where(full[:, None, :], gk, old))
            gi, ci = np.nonzero(got); gb[r][gi, :, (ak - (ak & (C - 1)))[gi, ci] + ci] = old[gi, :, ci]
            head[r] = np.where(got, (k + 1) & 15, np.where(full, 0, head[r])); wait[r] = np.where(full, 0, more)
            m[r] = int(np.count_nonzero(got)); a[r] = new
        h = np.stack([say[(r - 1 - t % (N - 1)) % N] for r in range(N)])
    return {"ys": a.reshape(N, 128, C).astype(np.float32), "yg": gb.reshape(N, 128, V).astype(np.float32), "yh": h.reshape(N, 128, C).astype(np.float32).astype(BF)}

@@ -1,0 +1,506 @@
+from concourse.mybir import AluOpType as A, ActivationFunctionType as F
+
+STEPS = 5
+FAR_ACT = False
+NQ = 2
+CH = 8 // NQ
+NG_ = 2
+PSPLIT = 4
+CA = 16 * CH
+
+SB = "sbuf"
+SCRATCH = {
+    "CU": (SB, [128, 4112], "bfloat16"), "XW0": (SB, [128, 4096], "bfloat16"), "XW1": (SB, [128, 4096], "bfloat16"),
+    "MX0": (SB, [128, 2048], "bfloat16"), "MX1": (SB, [128, 2048], "bfloat16"), "CX": (SB, [128, 8], "float32"),
+    "SI": (SB, [128, 2048], "int32"), "TB": (SB, [128, 18432], "float32"),
+    "AI": (SB, [128, 256], "int32"), "AH": (SB, [128, 512], "float16"), "YS": (SB, [128, 256], "float32"),
+    "HL": (SB, [128, 1536], "bfloat16"), "SP": (SB, [128, 1280], "bfloat16"),
+    "WT": (SB, [128, 8], "int32"), "WF": (SB, [128, 8], "float32"),
+    "ONE": (SB, [128, 256], "bfloat16"), "IW": (SB, [128, 160], "bfloat16"), "BO": (SB, [128, 128], "bfloat16"), "BO1": (SB, [128, 128], "bfloat16"),
+    "NI": (SB, [128, 128], "bfloat16"), "IDH": (SB, [128, 128], "float16"), "BM2": (SB, [128, 128], "bfloat16"), "I32K": (SB, [128, 128], "bfloat16"),
+    "E4": (SB, [128, 144], "bfloat16"), "EM2": (SB, [128, 144], "bfloat16"), "ET": (SB, [128, 2048], "bfloat16"),
+    "WB": (SB, [128, 128], "bfloat16"), "DG": (SB, [128, 128], "bfloat16"), "OM": (SB, [128, 128], "bfloat16"),
+    "SA": (SB, [128, 512], "float16"), "SS": (SB, [128, 512], "bfloat16"), "SD": (SB, [128, 512], "float16"),
+    "CK": (SB, [128, 128], "bfloat16"), "RS": (SB, [128, 128], "float32"),
+    "PI": (SB, [128, 8], "int32"), "COL": (SB, [128, 16], "float32"), "IR": (SB, [128, 128], "float32"), "LM": (SB, [128, 16], "float32"),
+    "CC": (SB, [128, 16], "float32"), "MC": (SB, [128, 24], "float32"),
+    "RR": (SB, [128, 256], "bfloat16"), "AT": (SB, [128, 256], "uint16"),
+    "YD": (SB, [128, 16, 16], "float16"), "YA": (SB, [128, 16, 16], "float16"), "YG": (SB, [128, 16, 16], "bfloat16"),
+    "SG": (SB, [128, 256], "bfloat16"), "FAR": (SB, [128, 256], "bfloat16"), "DZ": (SB, [128, 16, 16], "float16"), "KS": (SB, [128, 256], "float32"),
+    "KI": (SB, [128, 16], "int32"), "KK": (SB, [128, 16], "int32"), "OO": (SB, [128, 16], "int32"), "XX": (SB, [128, 16], "float32"),
+    "LL": (SB, [128, 2, 24], "int32"), "LU": (SB, [128, 32], "uint16"), "RQ": (SB, [128, 2, 16], "bfloat16"),
+    "DD": (SB, [128, 16], "float32"), "SW": (SB, [128, 16], "float32"), "ZB": (SB, [128, 16], "int32"), "ZC": (SB, [128, 16], "int32"), "LS": (SB, [128, 16], "uint16"),
+    "JJ": (SB, [128, 16], "float32"), "WN": (SB, [128, 16], "float32"), "TT": (SB, [128, 16], "float32"), "HH": (SB, [128, 16], "bfloat16"),
+    "P1": (SB, [128, 256], "float32"), "HM": (SB, [128, 256], "bfloat16"), "T1": (SB, [128, 256], "float32"), "T2": (SB, [128, 256], "float32"),
+    "XU": (SB, [128, 256], "bfloat16"),
+    "H40": ("psum", [128, 512], "float32"), "H41": ("psum", [128, 512], "float32"),
+    "PP0": ("psum", [128, 512], "float32"), "PP1": ("psum", [128, 512], "float32"),
+    "KP": ("psum", [128, 512], "float32"), "RP": ("psum", [128, 512], "float32"),
+    "X1": ("psum", [128, 512], "float32"), "X2": ("psum", [128, 32, 16], "float32"),
+    "OS": (SB, [128, 256], "float32"), "IF": (SB, [128, 128], "float32"),
+}
+DMAS = ["l_cu0", "l_cu1", "l_h", "l_a", "l_w", "l_t", "l_sp", "c_gap", "c_sw", "o_s0", "o_s1", "o_g", "o_h0", "o_h1"]
+SEMAPHORES = ["pe", "dve", "act", "pool", "sent"] + DMAS + ["ar%d_%d" % (t, h) for t in range(STEPS) for h in range(2)]
+
+COST = {"cyc": 1.0, "pe": 0.5, "gat": 1.56, "sca": 3.8, "fix": 15.0, "lat": 90.0, "own": 60.0, "dma": 2000.0, "bw": 200.0, "rem": 2200.0, "tt": 2.0}
+
+
+def build(g, T, topo, core):
+    rank = T.rank_of(core)
+    ranks = len(T.cores)
+    ops = []
+    tag = ["init"]
+    V, S, P = g.vector, g.scalar, g.tensor
+
+    def op(name, eng, fn, r, w, kind, n, bank=None):
+        ops.append({"name": name, "eng": eng, "fn": fn, "r": list(r), "w": list(w), "kind": kind, "n": n, "bank": bank, "tag": tag[0], "stop": False})
+
+    def vts(name, out, in0, s1, s2, o0, o1, r, w, n, bank=None):
+        if o1 is None:
+            op(name, "dve", lambda: V.tensor_scalar(out, in0, s1, None, o0), r, w, "el", n, bank)
+        else:
+            op(name, "dve", lambda: V.tensor_scalar(out, in0, s1, s2, o0, o1), r, w, "el", n, bank)
+
+    def vtt(name, out, a, b, o, r, w, n, bank=None, kind="el"):
+        op(name, "dve", lambda: V.tensor_tensor(out, a, b, o), r, w, kind, n, bank)
+
+    def vcp(name, out, a, r, w, n, bank=None, kind="el"):
+        op(name, "dve", lambda: V.tensor_copy(out, a), r, w, kind, n, bank)
+
+    def vset(name, out, c, w, n):
+        op(name, "dve", lambda: V.memset(out, c), [], w, "el", n)
+
+    def act(name, out, a, f, r, w, n, bank=None, kind="el", **kw):
+        op(name, "act", lambda: S.activation(out, a, f, **kw), r, w, kind, n, bank)
+
+    def mm(name, lst, r, w, bank):
+        if len(lst) > PSPLIT:
+            for j in range(0, len(lst), PSPLIT):
+                mm(name + "." + str(j), lst[j:j + PSPLIT], r, w, bank)
+            return
+
+        def fn():
+            last = None
+            for (o, l, x, st, sp, n) in lst:
+                last = P.matmul(o, l, x, st, sp)
+            return last
+        op(name, "pe", fn, r, w, "pe", sum(max(64, e[5]) for e in lst), bank)
+        ops[-1]["stop"] = lst[-1][4]
+
+    def dma(name, q, out, a, r, w, nbytes):
+        e = {"sync": g.sync, "act": g.scalar, "pool": g}[q]
+        op(name, q, lambda: e.dma_start(out, a), r, w, "dma", nbytes)
+
+    def pool(name, fn, r, w, n):
+        op(name, "pool", fn, r, w, "pool", n)
+
+    XW = [T.XW0, T.XW1]; MX = [T.MX0, T.MX1]; H4 = [T.H40, T.H41]; PP = [T.PP0, T.PP1]
+    ID = T.IW[:, 16:144]
+
+    dma("l_h", "sync", T.HL[:, 0:256], T.heard[:], [], ["h0_0", "h0_1"], 65536)
+    dma("l_a", "sync", T.AI[:], T.scroll[:], [], ["AI"], 131072)
+    dma("l_cu0", "sync", T.CU[:, 0:2048], T.cues[:, 2048:4096], [], ["CUa"], 524288)
+    dma("l_cu1", "sync", T.CU[:, 2048:4112], T.cues[:, 0:2064], [], ["CUb"], 524288)
+    dma("l_w", "act", T.WT[:, 0:1], T.w[:], [], ["WTw"], 4096)
+    dma("l_t", "act", T.WT[:, 4:5], T.th[:], [], ["WTt"], 4096)
+    dma("l_sp", "sync", T.SI[:], T.spare[:], [], ["SI"], 1048576)
+
+    vset("one", T.ONE[:, 0:128], 1.0, ["ONE"], 64)
+    vset("zero", T.ONE[:, 128:256], 0.0, ["ONEz"], 64)
+    vset("one2", T.IW[:], 1.0, ["IW"], 80)
+    pool("pi", lambda: g.iota(T.PI[:, 0:1], [[0, 1]], 0, 1), [], ["PI0"], 1)
+    pool("iw", lambda: g.affine_select(T.IW[:], T.IW[:], [[-1, 160]], A.is_equal, 0.0, 16, 1), ["IW"], ["IW"], 160)
+    pool("bo1", lambda: g.affine_select(T.BO1[:], T.ONE[:, 0:128], [[-16, 8], [0, 16]], A.is_ge, 0.0, 0, 1), ["ONE"], ["BO1"], 128)
+    pool("bo", lambda: g.affine_select(T.BO[:], T.BO1[:], [[16, 8], [0, 16]], A.is_ge, 0.0, 15, -1), ["BO1"], ["BO"], 128)
+    pool("ir", lambda: g.iota(T.IR[:], [[0, 8], [1, 16]], 0, 0, allow_small_or_imprecise_dtypes=True), [], ["IR"], 128)
+    pool("e1", lambda: g.affine_select(T.BO1[:], T.BO[:], [[0, 8], [1, 16]], A.is_equal, 0.0, -15, 0), ["BO"], ["BO1"], 128)
+    pool("cc", lambda: g.iota(T.CC[:], [[16, 16]], 0, 0, allow_small_or_imprecise_dtypes=True), [], ["CC"], 16)
+    vts("lane", T.PI[:, 2:3], T.PI[:, 0:1], 15, None, A.bitwise_and, None, ["PI0"], ["PI2"], 1)
+    vts("par", T.PI[:, 3:4], T.PI[:, 0:1], 4, 1, A.logical_shift_right, A.bitwise_and, ["PI0"], ["PI3"], 1)
+    vcp("lanef", T.COL[:, 0:2], T.PI[:, 2:4], ["PI2", "PI3"], ["C01"], 2)
+    LANE, ODD, EVEN = T.COL[:, 0:1], T.COL[:, 1:2], T.COL[:, 2:3]
+    vts("even", EVEN, ODD, -1.0, 1.0, A.mult, A.add, ["C01"], ["C2"], 1)
+    vts("dgc", T.COL[:, 3:4], LANE, 7.5, 4096.0, A.add, A.mult, ["C01"], ["C3"], 1)
+    vts("sgb", T.COL[:, 4:5], LANE, -1.0, 0.5, A.mult, A.add, ["C01"], ["C4"], 1)
+    vts("l16", T.COL[:, 5:6], LANE, 16.0, None, A.mult, None, ["C01"], ["C5"], 1)
+    pool("cx", lambda: g.iota(T.CX[:], [[256, 8]], 2048, 0, allow_small_or_imprecise_dtypes=True), [], ["CX"], 8)
+    vts("cx2", T.CX[:], T.CX[:], T.COL[:, 5:6], None, A.add, None, ["CX", "C5"], ["CX"], 8)
+    vcp("wf", T.WF[:, 0:1], T.WT[:, 0:1], ["WTw"], ["WFw"], 1)
+    FS = -1024.0 if FAR_ACT else 1.0
+    THR = T.MC[:, 20:21]
+    vts("thr", THR, T.WT[:, 4:5], 2.0 * FS, None, A.mult, None, ["WTt"], ["THR"], 1)
+    vts("tf", T.WF[:, 4:5], T.WT[:, 4:5], 7.5, 2.0 * FS, A.add, A.mult, ["WTt"], ["WFt"], 1)
+    vts("wb", T.WB[:], T.BO[:], T.WF[:, 0:1], None, A.mult, None, ["BO", "WFw"], ["WB"], 64)
+    vcp("idh", T.IDH[:], ID, ["IW"], ["IDH"], 64)
+    vcp("a0", T.AH[:, 0:256], T.AI[:], ["AI"], ["a0_0", "a0_1"], 256)
+    act("ni", T.NI[:], ID, F.Identity, ["IW"], ["NI"], 128, scale=-1.0)
+    vset("e4z", T.E4[:, 128:144], 0.0, ["E4z"], 8)
+    vset("em2z", T.EM2[:, 128:144], 0.0, ["EM2z"], 8)
+    act("e4", T.E4[:, 0:128], T.BO1[:], F.Identity, ["BO1"], ["E4"], 128, scale=4.0)
+    act("em2", T.EM2[:, 0:128], T.BO1[:], F.Identity, ["BO1"], ["EM2"], 128, scale=-2.0)
+    act("i32k", T.I32K[:], ID, F.Identity, ["IW"], ["I32K"], 128, scale=32768.0)
+    act("dg", T.DG[:], ID, F.Identity, ["IW", "C3"], ["DG"], 128, scale=T.COL[:, 3:4])
+    act("bm2", T.BM2[:], T.BO[:], F.Identity, ["BO"], ["BM2"], 128, scale=-2.0)
+    vset("om", T.OM[:], -1.0 / 4096.0, ["OM"], 64)
+    src = {0: (ID, EVEN), 1: (T.IW[:, 32:160], ODD), 2: (T.IW[:, 0:128], EVEN), 3: (ID, ODD)}
+    for j in range(4):
+        m, c = src[j]
+        vts("sd%d" % j, T.SD[:, 128 * j:128 * j + 128], m, c, 32768.0, A.mult, A.mult, ["IW", "C01", "C2"], ["SD%d" % j], 64)
+        vts("sa%d" % j, T.SA[:, 128 * j:128 * j + 128], m, c, None, A.mult, None, ["IW", "C01", "C2"], ["SA%d" % j], 64)
+        vts("ss%d" % j, T.SS[:, 128 * j:128 * j + 128], m, c, 16384.0, A.mult, A.mult, ["IW", "C01", "C2"], ["SS%d" % j], 64)
+    vts("lm", T.LM[:], T.IR[:, 0:16], LANE, -4096.0, A.is_equal, A.mult, ["IR", "C01"], ["LM"], 16)
+    for cl in range(16):
+        if cl % 2:
+            act("et%d" % cl, T.ET[:, 128 * cl:128 * cl + 128], T.BO[:], F.Identity, ["BO", "LM"], ["ET%d" % cl], 128, scale=T.LM[:, cl:cl + 1])
+        else:
+            vts("et%d" % cl, T.ET[:, 128 * cl:128 * cl + 128], T.BO[:], T.LM[:, cl:cl + 1], None, A.mult, None, ["BO", "LM"], ["ET%d" % cl], 64)
+    ETK = ["ET%d" % cl for cl in range(16)]
+    vset("ck0", T.CK[:], 0.0, ["CK"], 64)
+    vts("ck1", T.CK[0:32, :], T.IR[0:32, :], 8.0, 64.0, A.add, A.mult, ["IR"], ["CK"], 128)
+    vset("ck2", T.CK[32:64, :], -524288.0, ["CK"], 64)
+    vts("rs", T.RS[:], T.IR[:], 0.0, 67108864.0, A.is_equal, A.mult, ["IR"], ["RS"], 128)
+    vts("cc2", T.CC[:], T.CC[:], LANE, None, A.add, None, ["CC", "C01"], ["CC"], 16)
+    act("if", T.IF[:], ID, F.Identity, ["IW"], ["IF"], 128)
+    vset("sg0", T.SG[:], -1.0, ["SG"], 128)
+    vset("yg0", T.YG[:], -1.0, ["YG"], 128)
+    vset("sw0", T.SW[:], -0.5, ["SW"], 16)
+    vset("hh0", T.HH[:], -64.0, ["HH"], 16)
+    pool("sw_e", lambda: g.affine_select(T.XW0[:, 0:2048:2], T.CU[:, 2049:4096:2], [[0, 1024]], A.is_gt, 0.0, 1, 0), ["CUb"], ["SWe"], 1024)
+    pool("sw_o", lambda: g.affine_select(T.XW0[:, 1:2048:2], T.CU[:, 2048:4096:2], [[0, 1024]], A.is_gt, 0.0, 1, 0), ["CUb"], ["SWo"], 1024)
+    dma("c_sw", "sync", T.XW1[:, 0:2048], T.XW0[:, 0:2048], ["SWe", "SWo"], ["SW1"], 524288)
+    SWK = [["SWe", "SWo"], ["SW1"]]
+    pool("spf", lambda: g.affine_select(T.TB[:, 0:2048], T.SI[:], [[0, 2048]], A.is_gt, 0.0, 1, 0), ["SI"], ["spare"], 2048)
+    dma("c_gap", "sync", T.TB[:, 8192:10240], T.TB[:, 0:2048], ["spare"], ["gap"], 1048576)
+
+    def turn(out, mats, y, hf, names, hi=16, stop=False):
+        lst = []
+        for gw in range(2):
+            for gr in range(2):
+                j = 2 * gw + gr
+                lst.append((out[:, gr:8:2, 0:hi], mats[:, 128 * j:128 * j + 128], y[:, 8 * hf + gw:8 * hf + 8:2, 0:hi], False, False, 4 * hi))
+        return lst
+
+    def pre(t, hf):
+        c0 = 128 * hf
+        h = T.HL[:, 256 * t + c0:256 * t + c0 + 128]; hk = "h%d_%d" % (t, hf)
+        a = T.AH[:, 256 * (t % 2) + c0:256 * (t % 2) + c0 + 128]; ak = "a%d_%d" % (t % 2, hf)
+        u = "%d_%d" % (t, hf)
+        b1 = ("X1", "v" + u); ts = slice(8 * hf, 8 * hf + 8)
+        mm("v1" + u, [(T.X1[:, 0:128], T.IDH[:], a, True, False, 128), (T.X1[:, 0:128], T.WB[:], h, False, True, 128)], [hk, ak, "WB", "IDH"], [], b1)
+        act("rr" + u, T.RR[:, c0:c0 + 128], T.X1[:, 0:128], F.Identity, [], ["RR%d" % hf], 128, b1, bias=524288.0)
+        bh = ("H4%d" % hf, u); v2 = H4[hf][:, 128:256]
+        mm("v2" + u, [(H4[hf][:, 0:128], ID, h, True, True, 128), (v2, T.IDH[:], a, True, False, 128), (v2, T.WB[:], h, False, False, 128)], [hk, ak, "WB", "IDH", "IW"], [], bh)
+        mm("v3" + u, [(v2, T.NI[:], T.RR[:, c0:c0 + 128], False, True, 128)], ["RR%d" % hf, "NI"], [], bh)
+        vts("at" + u, T.AT[:, c0:c0 + 128], v2, 526336.0, None, A.add, None, [], ["AT%d" % hf], 128, bh)
+        op("ya" + u, "dve", lambda: V.transpose(T.YA[:, 8 * hf:8 * hf + 8, :], a), [ak], ["YA%d" % hf], "el", 64)
+
+    def heavy(t, hf):
+        c0 = 128 * hf
+        u = "%d_%d" % (t, hf)
+        h = T.HL[:, 256 * t + c0:256 * t + c0 + 128]; hk = "h%d_%d" % (t, hf)
+        X, M, Pm = XW[hf], MX[hf], PP[hf]
+        bh = ("H4%d" % hf, u); bp = ("PP%d" % hf, u)
+        mm("p0" + u, [(Pm[:, 0:128], T.BM2[:], h, True, False, 128)], ["BM2", hk], [], bp)
+        for q in range(NQ):
+            xk = ["x%d_%d_%d" % (hf, q, e) for e in range(NG_)]; w = u + "_%d" % q
+            cq = slice(CA * q, CA * q + CA); x0 = 2048 + 16 * CA * q
+            for e in range(NG_):
+                n = CA // NG_; b0 = CA * q + n * e
+                act("gg" + w + "_%d" % e, X[:, 2048 + 16 * b0:2048 + 16 * (b0 + n)], T.CU[:].indirect(T.AT[:, c0 + b0:c0 + b0 + n]), F.Copy,
+                    ["CUa", "CUb", "AT%d" % hf], [xk[e]], 16 * n, kind="gat")
+            mm("px" + w, [(Pm[:, cq], T.EM2[:, 15 - i:143 - i], X[:, x0 + i:x0 + 16 * CA:16], False, False, CA) for i in range(16)], xk + ["EM2", "EM2z"], [], bp)
+            for j in range(0, 16, 4):
+                for i in range(j, j + 4):
+                    vtt("mx" + w + "_%d" % i, M[:, 128 * i + CA * q:128 * i + CA * q + CA], X[:, x0 + i:x0 + 16 * CA:16], H4[hf][:, cq], A.max, xk, ["m%d_%d_%d" % (hf, q, i)], CA, bh)
+                mm("pm" + w + "_%d" % j, [(Pm[:, cq], T.E4[:, 15 - i:143 - i], M[:, 128 * i + CA * q:128 * i + CA * q + CA], False, q == NQ - 1 and i == 15, CA) for i in range(j, j + 4)],
+                   ["m%d_%d_%d" % (hf, q, i) for i in range(j, j + 4)] + ["E4", "E4z"], [], bp)
+
+    def post(t, hf):
+        c0 = 128 * hf; cs = slice(c0, c0 + 128); ts = slice(8 * hf, 8 * hf + 8)
+        u = "%d_%d" % (t, hf); f = "%d" % hf
+        h = T.HL[:, 256 * t + c0:256 * t + c0 + 128]; hk = "h%d_%d" % (t, hf)
+        a = T.AH[:, 256 * (t % 2) + c0:256 * (t % 2) + c0 + 128]; ak = "a%d_%d" % (t % 2, hf)
+        bp = ("PP%d" % hf, u); bk = ("KP", u); br = ("RP", u); bs = ("X1", "s" + u)
+        Pm = PP[hf]; K = T.KP[:, 0:128]
+        if FAR_ACT:
+            act("far" + u, T.FAR[:, cs], Pm[:, 0:128], F.Relu, ["THR"], ["FAR" + f], 128, bp, scale=1024.0, bias=THR)
+        else:
+            vts("far" + u, T.FAR[:, cs], Pm[:, 0:128], THR, 1024.0, A.is_gt, A.mult, ["THR"], ["FAR" + f], 128, bp)
+        for e in range(2):
+            vtt("dz" + u + "_%d" % e, T.DZ[:, 8 * hf + e:8 * hf + 8:2, :], Pm[:, 64 * e:64 * e + 64], T.FAR[:, c0 + 64 * e:c0 + 64 * e + 64], A.min, ["FAR" + f], ["DZ%d" % e + f], 64, bp)
+        op("yd" + u, "dve", lambda: V.transpose(T.YD[:, ts, :], T.DZ[:, ts, :]), ["DZ0" + f, "DZ1" + f], ["YD" + f], "el", 64)
+        bo = ("X2", "o" + u)
+        lst = [(T.X2[:, 0:8, :], T.ONE[:, 0:128], T.CK[:], True, False, 128)] + turn(T.X2, T.SS, T.YG, hf, None) + turn(T.X2, T.SA, T.YA, hf, None)
+        lst[-1] = lst[-1][0:4] + (True, lst[-1][5])
+        mm("o0" + u, lst, ["ONE", "CK", "YG", "YA" + f, "SS0", "SS1", "SS2", "SS3", "SA0", "SA1", "SA2", "SA3"], [], bo)
+        act("os" + u, T.OS[:, cs], T.X2[:, 0:8, :], F.Identity, [], ["OS" + f], 128, bo)
+        mm("k0" + u, [(K, T.IF[:], T.OS[:, cs], True, False, 512)], ["IF", "OS" + f], [], bk)
+        mm("k1" + u, [(T.KP[:, 64 * (j % 2):64 * (j % 2) + 64], T.SD[:, 128 * j:128 * j + 128], T.YD[:, 8 * hf + j // 2:8 * hf + 8:2, :], False, j == 3, 64) for j in range(4)],
+           ["YD" + f, "SD0", "SD1", "SD2", "SD3"], [], bk)
+        op("scan" + u, "dve", lambda: V.tensor_tensor_scan(T.KS[:, cs], T.RS[:], K, 0.0, A.add, A.min), ["RS"], ["KS" + f], "el", 128, bk)
+        km = T.KS[:, c0 + 15:c0 + 128:16]
+        N_, LP, Z = T.LL[:, hf, 0:8], T.LL[:, hf, 8:16], T.LL[:, hf, 16:24]
+        U, NG = T.RQ[:, hf, 0:8], T.RQ[:, hf, 8:16]
+        vcp("ki" + u, T.KI[:, ts], km, ["KS" + f], ["KI" + f], 8)
+        vts("ng" + u, NG, km, -16711680.0, 8192.0, A.is_ge, A.mult, ["KS" + f], ["NG" + f], 8)
+        vts("n" + u, N_, T.KI[:, ts], 2047, None, A.bitwise_and, None, ["KI" + f], ["N" + f], 8)
+        vts("o" + u, T.OO[:, ts], T.KI[:, ts], 11, 31, A.logical_shift_right, A.bitwise_and, ["KI" + f], ["OO" + f], 8)
+        vtt("z" + u, Z, N_, NG, A.add, ["N" + f, "NG" + f], ["Z" + f], 8)
+        vts("kk" + u, T.KK[:, ts], T.KI[:, ts], 11, 15, A.logical_shift_right, A.bitwise_and, ["KI" + f], ["KK" + f], 8)
+        vtt("x" + u, T.XX[:, ts], T.KK[:, ts], T.CX[:], A.add, ["KK" + f, "CX"], ["XX" + f], 8)
+        vtt("lp" + u, LP, T.XX[:, ts], Z, A.min, ["XX" + f, "Z" + f], ["LP" + f], 8)
+        lu = T.LU[:, 16 * hf:16 * hf + 16]
+        if t == 0:
+            vcp("lu" + u, lu, T.LL[:, hf, 0:16], ["N" + f, "LP" + f], ["LU" + f], 16)
+            lt_, lsp = T.LU[:, 16 * hf:16 * hf + 8], T.LU[:, 16 * hf + 8:16 * hf + 16]
+            win, wk = T.TB[:, 0:2048], ["spare"]
+        else:
+            vcp("lu" + u, lu, T.LL[:, hf, 8:24], ["Z" + f, "LP" + f], ["LU" + f], 16)
+            lsp, lt_ = T.LU[:, 16 * hf:16 * hf + 8], T.LU[:, 16 * hf + 8:16 * hf + 16]
+            win, wk = T.TB[:, 0:10240], ["spare", "gap"]
+        vtt("d" + u, T.DD[:, ts], NG, T.SW[:, ts], A.mult, ["NG" + f, "SW"], ["DD" + f], 8)
+        vtt("u" + u, U, T.OO[:, ts], T.DD[:, ts], A.add, ["OO" + f, "DD" + f], ["U" + f], 8)
+        mm("r0" + u, [(T.RP[:, 0:256], T.DG[:], T.ONE[:], True, False, 256), (T.RP[:, 0:128], T.I32K[:], T.SG[:, cs], False, False, 128),
+                      (T.RP[:, 128:256], ID, h, False, False, 128)], ["DG", "ONE", "ONEz", "I32K", "SG", "IW", hk], [], br)
+        mm("r1" + u, [(T.RP[:, cl:256:16], T.ET[:, 128 * cl:128 * cl + 128], T.RQ[:, hf, :], False, cl == 15, 16) for cl in range(16)], ETK + ["U" + f, "NG" + f], [], br)
+        act("hm" + u, T.HM[:, cs], T.RP[:, 128:256], F.Relu, [], ["HM" + f], 128, br)
+        act("p1" + u, T.P1[:, cs], T.RP[:, 0:128], F.Relu, [], ["P1" + f], 128, br, scale=-1.0)
+        vtt("t2" + u, T.T2[:, cs], a, T.RP[:, 0:128], A.min, [ak], ["T2" + f], 128, br)
+        act("xu" + u, T.XU[:, cs], XW[hf][:].indirect(lsp), F.Copy, SWK[hf] + ["x%d_%d_%d" % (hf, q, e) for q in range(NQ) for e in range(NG_)] + ["LU" + f], ["XU" + f], 128, kind="gat")
+        mm("s" + u, [(T.X1[:, 0:128], ID, T.XU[:, cs], True, False, 128), (T.X1[:, 0:128], T.NI[:], h, False, False, 128),
+                     (T.X1[:, 0:128], ID, T.HM[:, cs], False, True, 128)], ["XU" + f, "HM" + f, hk, "IW", "NI"], [], bs)
+        sp = T.SP[:, 256 * t + c0:256 * t + c0 + 128]
+        act("sp" + u, sp, T.X1[:, 0:128], F.Abs, [], ["sp" + u], 128, bs)
+        dst = T.cores[(rank + 1 + t % (ranks - 1)) % ranks]
+        rid, pid, _ = topo.addr(dst); mask = topo.mask(core, dst); ne = len(topo.engines(core, dst))
+        land = T.HL[:, 256 * (t + 1) + c0:256 * (t + 1) + c0 + 128]
+        op("send" + u, "pool", lambda: g.remote_dma(land, sp, T.sem["ar" + u], T.sem.sent, pid, rid, mask), ["sp" + u], ["snd" + u], "send", ne)
+        op("ar" + u, "net", None, ["snd" + u], ["h%d_%d" % (t + 1, hf)], "arr", ne)
+        vtt("t1" + u, T.T1[:, cs], win.indirect(lt_), T.P1[:, cs], A.min, wk + ["LU" + f, "P1" + f], ["T1" + f], 128, kind="gat")
+        if t < STEPS - 1:
+            na = T.AH[:, 256 * ((t + 1) % 2) + c0:256 * ((t + 1) % 2) + c0 + 128]
+            vtt("an" + u, na, T.T1[:, cs], T.T2[:, cs], A.max, ["T1" + f, "T2" + f], ["a%d_%d" % ((t + 1) % 2, hf)], 128, kind="tt")
+        else:
+            vtt("an" + u, T.YS[:, cs], T.T1[:, cs], T.T2[:, cs], A.max, ["T1" + f, "T2" + f], ["YS" + f], 128, kind="tt")
+            dma("o_s" + f, "sync", T.ys[:, cs], T.YS[:, cs], ["YS" + f], ["ys" + f], 65536)
+            dma("o_h" + f, "sync", T.yh[:, cs], land, ["h%d_%d" % (t + 1, hf)], ["yh" + f], 32768)
+
+    def both(t):
+        u = "%d" % t
+        vts("zb" + u, T.ZB[:], T.LL[:, :, 16:24], 0x2700, None, A.bitwise_and, None, ["Z0", "Z1"], ["ZB"], 16)
+        vtt("zc" + u, T.ZC[:], T.ZB[:], T.CC[:], A.add, ["ZB", "CC"], ["ZC"], 16)
+        vcp("ls" + u, T.LS[:], T.ZC[:], ["ZC"], ["LS"], 16)
+        a = T.AH[:, 256 * (t % 2):256 * (t % 2) + 256]
+        vcp("sc" + u, T.TB[:, 8192:18432].indirect(T.LS[:]), a, ["LS", "a%d_0" % (t % 2), "a%d_1" % (t % 2)], ["gap"], 256, kind="sca")
+        if t == STEPS - 1:
+            dma("o_g", "sync", T.yg[:], T.TB[:, 8192:10240], ["gap"], ["yg"], 1048576)
+            return
+        NG = T.RQ[:, :, 8:16]
+        bm = ("X2", "m" + u); bh = ("X2", "h" + u)
+        mm("mc" + u, [(T.X2[:, 0, :], T.OM[:], NG, True, True, 16)], ["OM", "NG0", "NG1"], [], bm)
+        act("ma" + u, T.MC[:, 0:16], T.X2[:, 0, :], F.Identity, [], ["MC"], 16, bm, scale=FS, bias=255.0625 * FS, accum_out=T.MC[:, 16:17])
+        vts("mr" + u, T.MC[:, 17:18], T.MC[:, 16:17], 402653184.0 * abs(FS), 402653184.0 * abs(FS), A.add, A.subtract, ["MC"], ["MR"], 1)
+        vts("thr" + u, THR, T.MC[:, 16:17], T.MC[:, 17:18], T.WF[:, 4:5], A.subtract, A.add, ["WFt", "MC", "MR"], ["THR"], 1)
+        vts("sw" + u, T.SW[:], T.DD[:], -1.0, 0.5, A.is_lt, A.subtract, ["DD0", "DD1"], ["SW"], 16)
+        vts("wn" + u, T.WN[:], T.DD[:], -1.0, 4096.0, A.is_ge, A.mult, ["DD0", "DD1"], ["WN"], 16)
+        vtt("j" + u, T.JJ[:], T.KK[:], NG, A.subtract, ["KK0", "KK1", "NG0", "NG1"], ["JJ"], 16)
+        vtt("tt" + u, T.TT[:], T.HH[:], T.WN[:], A.subtract, ["HH", "WN"], ["TT"], 16)
+        vtt("hh" + u, T.HH[:], T.JJ[:], T.TT[:], A.max, ["JJ", "TT"], ["HH"], 16)
+        mm("hr" + u, [(T.X2[:, 0:16, cl], T.ET[:, 128 * cl:128 * cl + 128], T.HH[:], True, True, 16) for cl in range(16)], ETK + ["HH"], [], bh)
+        act("sg" + u, T.SG[:], T.X2[:, 0:16, :], F.Sign, ["C4"], ["SG"], 256, bh, scale=-1.0 / 4096.0, bias=T.COL[:, 4:5])
+        op("yg" + u, "dve", lambda: V.transpose(T.YG[:], T.SG[:]), ["SG"], ["YG"], "el", 128)
+
+    for t in range(STEPS):
+        for part in (("pre", pre), ("heavy", heavy), ("post", post)):
+            for hf in range(2):
+                tag[0] = part[0] + str(hf)
+                part[1](t, hf)
+        tag[0] = "both"
+        both(t)
+    return ops
+
+
+def cost(o, c):
+    k, n = o["kind"], o["n"]
+    if k == "pe":
+        return 10.0 + n * c["pe"]
+    if k == "el":
+        return c["fix"] + max(n, 64) * c["cyc"]
+    if k == "tt":
+        return c["fix"] + n * c["tt"] * c["cyc"]
+    if k == "gat":
+        return 60.0 + n * c["gat"] * c["cyc"]
+    if k == "sca":
+        return 60.0 + n * c["sca"] * c["cyc"]
+    if k == "pool":
+        return 170.0 + 2 * n * c["cyc"]
+    if k == "dma":
+        return 60.0
+    if k == "send":
+        return 300.0
+    return 0.0
+
+
+ORDERED = ("KP", "RP", "H40", "H41", "PP0", "PP1")
+
+
+def depend(ops):
+    writer, readers, sess, lastof = {}, {}, {}, {}
+    for i, o in enumerate(ops):
+        d = set()
+        for k in o["r"]:
+            if k in writer:
+                d.add(writer[k])
+        for k in o["w"]:
+            if k in writer:
+                d.add(writer[k])
+            d.update(readers.get(k, []))
+        for k in o["r"]:
+            readers.setdefault(k, []).append(i)
+        for k in o["w"]:
+            writer[k] = i
+            readers[k] = []
+        b = o["bank"]
+        if b is not None:
+            if b in sess:
+                d.update(j for j in sess[b] if j == sess[b][0] or o["stop"] or ops[j]["eng"] != o["eng"])
+            elif b[0] in ORDERED and b[0] in lastof:
+                d.update(sess[lastof[b[0]]])
+            sess.setdefault(b, []).append(i)
+            lastof[b[0]] = b
+        d.discard(i)
+        o["dep"] = d
+    return sess
+
+
+def finish(o, start, c, dmafree):
+    if o["kind"] == "dma":
+        s = max(start + c["dma"] * 0.6, dmafree[0])
+        dmafree[0] = s + o["n"] / c["bw"]
+        return dmafree[0] + c["dma"] * 0.4
+    if o["kind"] == "arr":
+        return start + c["rem"]
+    return start + cost(o, c)
+
+
+def soft(o, p):
+    if o["eng"] != p["eng"]:
+        return False
+    if o["eng"] == "pe":
+        return True
+    if o["bank"] is not None and p["bank"] is not None and o["bank"][0] == p["bank"][0]:
+        return not (set(o["r"]) & set(p["w"]) or set(o["w"]) & set(p["r"]) or set(o["w"]) & set(p["w"]))
+    return False
+
+
+def ready_at(ops, o, end, free, c):
+    s = free.get(o["eng"], 0.0)
+    for j in o["dep"]:
+        p = ops[j]
+        if soft(o, p):
+            continue
+        s = max(s, end[j] + (c["own"] if p["eng"] == o["eng"] else c["lat"]))
+    return s
+
+
+TUNE = {'slack': 30.0, 'lam': 20, 'l_h': 200000.0, 'l_a': 100000.0, 'pre0': 4700.0, 'post0': 3100.0, 'both': 600.0, 'heavy1': -1800.0, 'rr:pre0': 2000.0, 'o_:post1': 800.0, 'lu:post0': -2400.0, 'hh:both': -1000.0, 'v1:pre0': 6300.0, 'p0:heavy0': -2200.0, 'mc:both': -2200.0, 'sp:post1': 1300.0, 'sc:post1': -1000.0, 'pm:heavy0': -1000.0, 'px:heavy0': 1700.0, 'yd:post0': 400.0, 'xu:post0': 6000.0, 'sp:post0': 4100.0, 'ar:post0': 9100.0, 'p1:post1': 900.0, 'v2:pre0': -1300.0, 'ls:both': -3700.0, 'k0:post1': -200.0, 'k0:post0': -200.0, 'an:post0': 3000.0, 'o_:post0': -7200.0, 'dz:post0': 1500.0, 'rr:pre1': -20000.0, 'pre1': 13400.0, 'lp:post1': -1500.0, 't2:post0': 8700.0, 'at:pre1': -400.0, 'pm:heavy1': -5600.0, 'sw:both': 300.0, 'v3:pre0': 14300.0, 'yg:both': 5000.0, 'ma:both': 600.0, 'p0:heavy1': -1100.0, 'k1:post1': 2300.0, 'lp:post0': 3800.0, 'se:post0': 6200.0, 'ar:post1': -6300.0, 'v2:pre1': -600.0, 'mx:heavy0': -2400.0, 'fa:post1': 6500.0, 'lu:post1': -3700.0, 'wn:both': 900.0, 'kk:post1': -2400.0, 'mr:both': -500.0, 'sg:both': -400.0, 'r1:post0': -1100.0, 'hr:both': 7600.0, 'fa:post0': -2100.0, 'ng:post1': -600.0, 'v3:pre1': 400.0, 'sc:post0': 4700.0, 'r1:post1': -2600.0, 'r0:post1': 10400.0, 'os:post1': -2500.0, 't1:post1': -300.0, 'ya:pre1': -2200.0, 'ki:post0': -1300.0, 'dz:post1': 600.0, 'zc:both': 1000.0, 'zb:both': -900.0, 't1:post0': 1200.0, 'heavy0': -700.0, 'ng:post0': -1200.0, 'k1:post0': 4300.0, 'ki:post1': -1900.0, 'mx:heavy1': -400.0, 'kk:post0': 300.0, 'th:both': 2200.0, 'o_:both': -500.0, 'sc:both': 700.0, 'px:heavy1': -1000.0, 'post1': -700.0, 'hm:post1': 1500.0, 'ya:pre0': -2800.0, 'yd:post1': 1100.0, 'os:post0': -1600.0, 'gg:heavy1': 2200.0, 'se:post1': 700.0, 'p1:post0': -400.0, 'xu:post1': 2800.0, 'hm:post0': 3600.0, 'tt:both': 1500.0}
+
+
+def tune(o):
+    kind = o["name"][:2] + ":" + o["tag"]
+    return TUNE.get(o["tag"], 0.0) + TUNE.get(o["name"], 0.0) + TUNE.get(kind, 0.0)
+
+
+def schedule(ops, c):
+    sess = depend(ops)
+    n = len(ops)
+    succ = [[] for _ in range(n)]
+    for i, o in enumerate(ops):
+        for j in o["dep"]:
+            succ[j].append(i)
+    prio = [0.0] * n
+    for i in range(n - 1, -1, -1):
+        own = finish(ops[i], 0.0, c, [0.0]) + c["lat"]
+        prio[i] = own + max([prio[j] for j in succ[i]] + [0.0])
+    for i in range(n):
+        prio[i] += tune(ops[i])
+    left = [len(o["dep"]) for o in ops]
+    ready = [i for i in range(n) if left[i] == 0]
+    end, free, order, holder, done = {}, {}, [], {}, set()
+    dmafree = [0.0]
+    while ready:
+        cand = []
+        for i in ready:
+            o = ops[i]; b = o["bank"]
+            extra = []
+            if b is not None and b[0] not in ORDERED and sess[b][0] == i and b[0] in holder:
+                extra = sess[holder[b[0]]]
+                if any(j not in done for j in extra):
+                    continue
+            keep = o["dep"]
+            o["dep"] = keep | set(extra)
+            cand.append((ready_at(ops, o, end, free, c), i, extra))
+            o["dep"] = keep
+        first = min(cand)
+        eng = ops[first[1]]["eng"]
+        s, i, extra = max((e for e in cand if ops[e[1]]["eng"] == eng and e[0] <= first[0] + TUNE["slack"]), key=lambda e: (prio[e[1]] - TUNE["lam"] * e[0], -e[1]))
+        o = ops[i]
+        o["dep"] = o["dep"] | set(extra)
+        if o["bank"] is not None:
+            holder[o["bank"][0]] = o["bank"]
+        end[i] = finish(o, s, c, dmafree)
+        if o["eng"] != "net":
+            free[o["eng"]] = s + cost(o, c)
+        o["t"] = (s, end[i])
+        order.append(i); done.add(i); ready.remove(i)
+        for j in succ[i]:
+            left[j] -= 1
+            if left[j] == 0:
+                ready.append(j)
+    assert len(order) == n
+    return order
+
+
+def emit(g, T, ops, order):
+    q = {"pe": g.tensor, "dve": g.vector, "act": g.scalar, "pool": g, "sync": g.sync}
+    count = {"pe": 0, "dve": 0, "act": 0, "pool": 0}
+    mark, seen, sent = {}, {e: {} for e in q}, 0
+    needed = set()
+    for i in order:
+        for j in ops[i]["dep"]:
+            if not soft(ops[i], ops[j]):
+                needed.add(j)
+    for i in order:
+        o = ops[i]; e = o["eng"]
+        if e == "net":
+            mark[i] = (o["name"], o["n"])
+            continue
+        want = {}
+        for j in o["dep"]:
+            if j in mark and not soft(o, ops[j]):
+                s, v = mark[j]
+                want[s] = max(want.get(s, 0), v)
+        for s in sorted(want):
+            if seen[e].get(s, 0) < want[s]:
+                q[e].wait_ge(T.sem[s], want[s])
+                seen[e][s] = want[s]
+        ins = o["fn"]()
+        if o["kind"] == "dma":
+            ins.then_inc(T.sem[o["name"]], 16)
+            mark[i] = (o["name"], 16)
+        elif o["kind"] == "send":
+            sent += o["n"]
+        elif i in needed:
+            count[e] += 1
+            ins.then_inc(T.sem[e], 1)
+            mark[i] = (e, count[e])
+    g.wait_ge(T.sem.sent, sent)
+    for s in ["o_s0", "o_s1", "o_h0", "o_h1", "o_g"]:
+        g.wait_ge(T.sem[s], 16)
+
+
+def rank_program(g, core, T, topo):
+    if T.rank_of(core) is None:
+        return
+    ops = build(g, T, topo, core)
+    emit(g, T, ops, schedule(ops, COST))

@@ -1,59 +1,64 @@
 from concourse.mybir import AluOpType as A, ActivationFunctionType as F
 
 STEPS = 5
-FAR_ACT = False
-NQ = 2
-CH = 8 // NQ
-NG_ = 2
-PSPLIT = 4
-CA = 16 * CH
+OPT = {
+    "gat": [32, 32, 32, 32],
+    "mx": [64, 32, 32],
+    "pm": [64, 64],
+    "rr": "act",
+    "speech": "dve",
+    "conv": 4,
+}
 
 SB = "sbuf"
 SCRATCH = {
-    "CU": (SB, [128, 4112], "bfloat16"), "XW0": (SB, [128, 4096], "bfloat16"), "XW1": (SB, [128, 4096], "bfloat16"),
-    "MX0": (SB, [128, 2048], "bfloat16"), "MX1": (SB, [128, 2048], "bfloat16"), "CX": (SB, [128, 8], "float32"),
-    "SI": (SB, [128, 2048], "int32"), "TB": (SB, [128, 18432], "float32"),
+    "CU": (SB, [128, 4096], "bfloat16"), "XW0": (SB, [128, 4096], "bfloat16"), "XW1": (SB, [128, 4096], "bfloat16"),
+    "MX0": (SB, [128, 2048], "bfloat16"), "MX1": (SB, [128, 2048], "bfloat16"),
+    "TB": (SB, [128, 10240], "int32"), "GO": (SB, [128, 6144], "float32"),
     "AI": (SB, [128, 256], "int32"), "AH": (SB, [128, 512], "float16"), "YS": (SB, [128, 256], "float32"),
     "HL": (SB, [128, 1536], "bfloat16"), "SP": (SB, [128, 1280], "bfloat16"),
     "WT": (SB, [128, 8], "int32"), "WF": (SB, [128, 8], "float32"),
-    "ONE": (SB, [128, 256], "bfloat16"), "IW": (SB, [128, 160], "bfloat16"), "BO": (SB, [128, 128], "bfloat16"), "BO1": (SB, [128, 128], "bfloat16"),
-    "NI": (SB, [128, 128], "bfloat16"), "IDH": (SB, [128, 128], "float16"), "BM2": (SB, [128, 128], "bfloat16"), "I32K": (SB, [128, 128], "bfloat16"),
+    "ONE": (SB, [128, 128], "bfloat16"), "IW": (SB, [128, 160], "bfloat16"), "BO": (SB, [128, 128], "bfloat16"), "BO1": (SB, [128, 128], "bfloat16"),
+    "NI": (SB, [128, 128], "bfloat16"), "IDH": (SB, [128, 128], "float16"), "BM2": (SB, [128, 128], "bfloat16"), "I8": (SB, [128, 128], "bfloat16"),
     "E4": (SB, [128, 144], "bfloat16"), "EM2": (SB, [128, 144], "bfloat16"), "ET": (SB, [128, 2048], "bfloat16"),
-    "WB": (SB, [128, 128], "bfloat16"), "DG": (SB, [128, 128], "bfloat16"), "OM": (SB, [128, 128], "bfloat16"),
+    "WB": (SB, [128, 128], "bfloat16"), "OM": (SB, [128, 128], "bfloat16"),
     "SA": (SB, [128, 512], "float16"), "SS": (SB, [128, 512], "bfloat16"), "SD": (SB, [128, 512], "float16"),
     "CK": (SB, [128, 128], "bfloat16"), "RS": (SB, [128, 128], "float32"),
     "PI": (SB, [128, 8], "int32"), "COL": (SB, [128, 16], "float32"), "IR": (SB, [128, 128], "float32"), "LM": (SB, [128, 16], "float32"),
-    "CC": (SB, [128, 16], "float32"), "MC": (SB, [128, 24], "float32"),
+    "CC": (SB, [128, 16], "float32"), "CX": (SB, [128, 8], "float32"), "MC": (SB, [128, 24], "float32"),
     "RR": (SB, [128, 256], "bfloat16"), "AT": (SB, [128, 256], "uint16"),
     "YD": (SB, [128, 16, 16], "float16"), "YA": (SB, [128, 16, 16], "float16"), "YG": (SB, [128, 16, 16], "bfloat16"),
-    "SG": (SB, [128, 256], "bfloat16"), "FAR": (SB, [128, 256], "bfloat16"), "DZ": (SB, [128, 16, 16], "float16"), "KS": (SB, [128, 256], "float32"),
-    "KI": (SB, [128, 16], "int32"), "KK": (SB, [128, 16], "int32"), "OO": (SB, [128, 16], "int32"), "XX": (SB, [128, 16], "float32"),
-    "LL": (SB, [128, 2, 24], "int32"), "LU": (SB, [128, 32], "uint16"), "RQ": (SB, [128, 2, 16], "bfloat16"),
-    "DD": (SB, [128, 16], "float32"), "SW": (SB, [128, 16], "float32"), "ZB": (SB, [128, 16], "int32"), "ZC": (SB, [128, 16], "int32"), "LS": (SB, [128, 16], "uint16"),
-    "JJ": (SB, [128, 16], "float32"), "WN": (SB, [128, 16], "float32"), "TT": (SB, [128, 16], "float32"), "HH": (SB, [128, 16], "bfloat16"),
-    "P1": (SB, [128, 256], "float32"), "HM": (SB, [128, 256], "bfloat16"), "T1": (SB, [128, 256], "float32"), "T2": (SB, [128, 256], "float32"),
-    "XU": (SB, [128, 256], "bfloat16"),
-    "H40": ("psum", [128, 512], "float32"), "H41": ("psum", [128, 512], "float32"),
-    "PP0": ("psum", [128, 512], "float32"), "PP1": ("psum", [128, 512], "float32"),
-    "KP": ("psum", [128, 512], "float32"), "RP": ("psum", [128, 512], "float32"),
-    "X1": ("psum", [128, 512], "float32"), "X2": ("psum", [128, 32, 16], "float32"),
-    "OS": (SB, [128, 256], "float32"), "IF": (SB, [128, 128], "float32"),
+    "SG": (SB, [128, 256], "bfloat16"), "FAR": (SB, [128, 256], "bfloat16"), "DZ": (SB, [128, 256], "float16"), "KS": (SB, [128, 128, 2], "float32"),
+    "KI": (SB, [128, 16], "int32"), "LL": (SB, [128, 2, 5, 8], "int32"), "RQ": (SB, [128, 2, 5, 8], "bfloat16"), "LU": (SB, [128, 32], "uint16"),
+    "SW": (SB, [128, 16], "float32"), "ZB": (SB, [128, 16], "int32"), "ZC": (SB, [128, 16], "int32"), "LS": (SB, [128, 16], "uint16"),
+    "TT": (SB, [128, 16], "float32"), "HH": (SB, [128, 16], "bfloat16"),
+    "P1": (SB, [128, 256], "bfloat16"), "HM": (SB, [128, 256], "bfloat16"), "T1": (SB, [128, 256], "float32"), "XU": (SB, [128, 256], "bfloat16"),
+    "H0": ("psum", [128, 128, 4], "float32"), "H1": ("psum", [128, 128, 4], "float32"),
+    "P0": ("psum", [128, 512], "float32"), "P1b": ("psum", [128, 512], "float32"),
+    "K0": ("psum", [128, 512], "float32"), "K1": ("psum", [128, 512], "float32"),
+    "X2": ("psum", [128, 32, 16], "float32"),
 }
-DMAS = ["l_cu0", "l_cu1", "l_h", "l_a", "l_w", "l_t", "l_sp", "c_gap", "c_sw", "o_s0", "o_s1", "o_g", "o_h0", "o_h1"]
+DMAS = ["l_cu0", "l_cu1", "l_h", "l_a", "l_w", "l_t", "l_sp", "l_gap", "c_sw", "o_s0", "o_s1", "o_g", "o_h0", "o_h1"]
 SEMAPHORES = ["pe", "dve", "act", "pool", "sent"] + DMAS + ["ar%d_%d" % (t, h) for t in range(STEPS) for h in range(2)]
 
-COST = {"cyc": 1.0, "pe": 0.5, "gat": 1.56, "sca": 3.8, "fix": 15.0, "lat": 90.0, "own": 60.0, "dma": 2000.0, "bw": 200.0, "rem": 2200.0, "tt": 2.0}
+COST = {"cyc": 0.9, "pe": 0.45, "gat": 1.56, "sca": 3.8, "fix": 30.0, "lat": 150.0, "own": 100.0, "dma": 2000.0, "bw": 250.0, "rem": 2500.0, "send": 300.0}
+
+
+def cuts(sizes):
+    out, s = [], 0
+    for n in sizes:
+        out.append((s, n)); s += n
+    return out
 
 
 def build(g, T, topo, core):
     rank = T.rank_of(core)
     ranks = len(T.cores)
     ops = []
-    tag = ["init"]
     V, S, P = g.vector, g.scalar, g.tensor
 
     def op(name, eng, fn, r, w, kind, n, bank=None):
-        ops.append({"name": name, "eng": eng, "fn": fn, "r": list(r), "w": list(w), "kind": kind, "n": n, "bank": bank, "tag": tag[0], "stop": False})
+        ops.append({"name": name, "eng": eng, "fn": fn, "r": list(r), "w": list(w), "kind": kind, "n": n, "bank": bank, "stop": False})
 
     def vts(name, out, in0, s1, s2, o0, o1, r, w, n, bank=None):
         if o1 is None:
@@ -70,13 +75,16 @@ def build(g, T, topo, core):
     def vset(name, out, c, w, n):
         op(name, "dve", lambda: V.memset(out, c), [], w, "el", n)
 
+    def vtr(name, out, a, r, w, n):
+        op(name, "dve", lambda: V.transpose(out, a), r, w, "el", n)
+
     def act(name, out, a, f, r, w, n, bank=None, kind="el", **kw):
         op(name, "act", lambda: S.activation(out, a, f, **kw), r, w, kind, n, bank)
 
-    def mm(name, lst, r, w, bank):
-        if len(lst) > PSPLIT:
-            for j in range(0, len(lst), PSPLIT):
-                mm(name + "." + str(j), lst[j:j + PSPLIT], r, w, bank)
+    def mm(name, lst, r, w, bank, piece=4):
+        if len(lst) > piece:
+            for j in range(0, len(lst), piece):
+                mm(name + "." + str(j), lst[j:j + piece], r, w, bank, piece)
             return
 
         def fn():
@@ -94,61 +102,60 @@ def build(g, T, topo, core):
     def pool(name, fn, r, w, n):
         op(name, "pool", fn, r, w, "pool", n)
 
-    XW = [T.XW0, T.XW1]; MX = [T.MX0, T.MX1]; H4 = [T.H40, T.H41]; PP = [T.PP0, T.PP1]
+    XW = [T.XW0, T.XW1]; MX = [T.MX0, T.MX1]; HB = [T.H0, T.H1]; PB = [T.P0, T.P1b]; KB = [T.K0, T.K1]
     ID = T.IW[:, 16:144]
 
-    dma("l_h", "sync", T.HL[:, 0:256], T.heard[:], [], ["h0_0", "h0_1"], 65536)
-    dma("l_a", "sync", T.AI[:], T.scroll[:], [], ["AI"], 131072)
-    dma("l_cu0", "sync", T.CU[:, 0:2048], T.cues[:, 2048:4096], [], ["CUa"], 524288)
-    dma("l_cu1", "sync", T.CU[:, 2048:4112], T.cues[:, 0:2064], [], ["CUb"], 524288)
     dma("l_w", "act", T.WT[:, 0:1], T.w[:], [], ["WTw"], 4096)
     dma("l_t", "act", T.WT[:, 4:5], T.th[:], [], ["WTt"], 4096)
-    dma("l_sp", "sync", T.SI[:], T.spare[:], [], ["SI"], 1048576)
+    dma("l_h", "sync", T.HL[:, 0:256], T.heard[:], [], ["h0_0", "h0_1", "q0"], 65536)
+    dma("l_a", "sync", T.AI[:], T.scroll[:], ["q0"], ["AI", "q1"], 131072)
+    dma("l_cu1", "sync", T.CU[:, 2048:4096], T.cues[:, 0:2048], ["q1"], ["CUb", "q2"], 524288)
+    dma("l_cu0", "sync", T.CU[:, 0:2048], T.cues[:, 2048:4096], ["q2"], ["CUa", "q3"], 524288)
+    dma("l_sp", "sync", T.TB[:, 0:2048], T.spare[:], ["q3"], ["spare", "q4"], 1048576)
 
-    vset("one", T.ONE[:, 0:128], 1.0, ["ONE"], 64)
-    vset("zero", T.ONE[:, 128:256], 0.0, ["ONEz"], 64)
+    vset("one", T.ONE[:], 1.0, ["ONE"], 64)
     vset("one2", T.IW[:], 1.0, ["IW"], 80)
     pool("pi", lambda: g.iota(T.PI[:, 0:1], [[0, 1]], 0, 1), [], ["PI0"], 1)
-    pool("iw", lambda: g.affine_select(T.IW[:], T.IW[:], [[-1, 160]], A.is_equal, 0.0, 16, 1), ["IW"], ["IW"], 160)
-    pool("bo1", lambda: g.affine_select(T.BO1[:], T.ONE[:, 0:128], [[-16, 8], [0, 16]], A.is_ge, 0.0, 0, 1), ["ONE"], ["BO1"], 128)
+    pool("bo1", lambda: g.affine_select(T.BO1[:], T.ONE[:], [[-16, 8], [0, 16]], A.is_ge, 0.0, 0, 1), ["ONE"], ["BO1"], 128)
     pool("bo", lambda: g.affine_select(T.BO[:], T.BO1[:], [[16, 8], [0, 16]], A.is_ge, 0.0, 15, -1), ["BO1"], ["BO"], 128)
+    pool("iw", lambda: g.affine_select(T.IW[:], T.IW[:], [[-1, 160]], A.is_equal, 0.0, 16, 1), ["IW"], ["IW"], 160)
     pool("ir", lambda: g.iota(T.IR[:], [[0, 8], [1, 16]], 0, 0, allow_small_or_imprecise_dtypes=True), [], ["IR"], 128)
-    pool("e1", lambda: g.affine_select(T.BO1[:], T.BO[:], [[0, 8], [1, 16]], A.is_equal, 0.0, -15, 0), ["BO"], ["BO1"], 128)
     pool("cc", lambda: g.iota(T.CC[:], [[16, 16]], 0, 0, allow_small_or_imprecise_dtypes=True), [], ["CC"], 16)
     vts("lane", T.PI[:, 2:3], T.PI[:, 0:1], 15, None, A.bitwise_and, None, ["PI0"], ["PI2"], 1)
     vts("par", T.PI[:, 3:4], T.PI[:, 0:1], 4, 1, A.logical_shift_right, A.bitwise_and, ["PI0"], ["PI3"], 1)
     vcp("lanef", T.COL[:, 0:2], T.PI[:, 2:4], ["PI2", "PI3"], ["C01"], 2)
     LANE, ODD, EVEN = T.COL[:, 0:1], T.COL[:, 1:2], T.COL[:, 2:3]
     vts("even", EVEN, ODD, -1.0, 1.0, A.mult, A.add, ["C01"], ["C2"], 1)
-    vts("dgc", T.COL[:, 3:4], LANE, 7.5, 4096.0, A.add, A.mult, ["C01"], ["C3"], 1)
+    vts("dgc", T.COL[:, 3:4], LANE, 7.5, -4096.0, A.add, A.mult, ["C01"], ["C3"], 1)
     vts("sgb", T.COL[:, 4:5], LANE, -1.0, 0.5, A.mult, A.add, ["C01"], ["C4"], 1)
-    vts("l16", T.COL[:, 5:6], LANE, 16.0, None, A.mult, None, ["C01"], ["C5"], 1)
-    pool("cx", lambda: g.iota(T.CX[:], [[256, 8]], 2048, 0, allow_small_or_imprecise_dtypes=True), [], ["CX"], 8)
-    vts("cx2", T.CX[:], T.CX[:], T.COL[:, 5:6], None, A.add, None, ["CX", "C5"], ["CX"], 8)
+    vts("cc2", T.CC[:], T.CC[:], LANE, None, A.add, None, ["CC", "C01"], ["CC"], 16)
+    for hf in range(2):
+        vts("cx%d" % hf, T.RQ[:, hf, 3, :], T.CC[:, 0:8], 128.0, 16.0, A.add, A.mult, ["CC"], ["CX%d" % hf], 8)
     vcp("wf", T.WF[:, 0:1], T.WT[:, 0:1], ["WTw"], ["WFw"], 1)
-    FS = -1024.0 if FAR_ACT else 1.0
     THR = T.MC[:, 20:21]
-    vts("thr", THR, T.WT[:, 4:5], 2.0 * FS, None, A.mult, None, ["WTt"], ["THR"], 1)
-    vts("tf", T.WF[:, 4:5], T.WT[:, 4:5], 7.5, 2.0 * FS, A.add, A.mult, ["WTt"], ["WFt"], 1)
+    vts("thr", THR, T.WT[:, 4:5], 2.0, None, A.mult, None, ["WTt"], ["THR"], 1)
+    vts("tf", T.WF[:, 4:5], T.WT[:, 4:5], 7.5, 2.0, A.add, A.mult, ["WTt"], ["WFt"], 1)
     vts("wb", T.WB[:], T.BO[:], T.WF[:, 0:1], None, A.mult, None, ["BO", "WFw"], ["WB"], 64)
     vcp("idh", T.IDH[:], ID, ["IW"], ["IDH"], 64)
-    vcp("a0", T.AH[:, 0:256], T.AI[:], ["AI"], ["a0_0", "a0_1"], 256)
+    for hf in range(2):
+        vcp("a0%d" % hf, T.AH[:, 128 * hf:128 * hf + 128], T.AI[:, 128 * hf:128 * hf + 128], ["AI"], ["a0_%d" % hf], 128)
     act("ni", T.NI[:], ID, F.Identity, ["IW"], ["NI"], 128, scale=-1.0)
     vset("e4z", T.E4[:, 128:144], 0.0, ["E4z"], 8)
     vset("em2z", T.EM2[:, 128:144], 0.0, ["EM2z"], 8)
+    vts("e1", T.BO1[:], T.IR[:], 15.0, None, A.is_equal, None, ["IR", "BO"], ["BO1"], 128)
+    vtt("e2", T.BO1[:], T.BO1[:], T.BO[:], A.mult, ["BO1", "BO"], ["BO1"], 256)
     act("e4", T.E4[:, 0:128], T.BO1[:], F.Identity, ["BO1"], ["E4"], 128, scale=4.0)
     act("em2", T.EM2[:, 0:128], T.BO1[:], F.Identity, ["BO1"], ["EM2"], 128, scale=-2.0)
-    act("i32k", T.I32K[:], ID, F.Identity, ["IW"], ["I32K"], 128, scale=32768.0)
-    act("dg", T.DG[:], ID, F.Identity, ["IW", "C3"], ["DG"], 128, scale=T.COL[:, 3:4])
+    act("i8", T.I8[:], ID, F.Identity, ["IW"], ["I8"], 128, scale=8.0)
     act("bm2", T.BM2[:], T.BO[:], F.Identity, ["BO"], ["BM2"], 128, scale=-2.0)
-    vset("om", T.OM[:], -1.0 / 4096.0, ["OM"], 64)
+    vset("om", T.OM[:], -1.0 / 2048.0, ["OM"], 64)
     src = {0: (ID, EVEN), 1: (T.IW[:, 32:160], ODD), 2: (T.IW[:, 0:128], EVEN), 3: (ID, ODD)}
     for j in range(4):
         m, c = src[j]
         vts("sd%d" % j, T.SD[:, 128 * j:128 * j + 128], m, c, 32768.0, A.mult, A.mult, ["IW", "C01", "C2"], ["SD%d" % j], 64)
         vts("sa%d" % j, T.SA[:, 128 * j:128 * j + 128], m, c, None, A.mult, None, ["IW", "C01", "C2"], ["SA%d" % j], 64)
         vts("ss%d" % j, T.SS[:, 128 * j:128 * j + 128], m, c, 16384.0, A.mult, A.mult, ["IW", "C01", "C2"], ["SS%d" % j], 64)
-    vts("lm", T.LM[:], T.IR[:, 0:16], LANE, -4096.0, A.is_equal, A.mult, ["IR", "C01"], ["LM"], 16)
+    vts("lm", T.LM[:], T.IR[:, 0:16], LANE, -1.0, A.is_equal, A.mult, ["IR", "C01"], ["LM"], 16)
     for cl in range(16):
         if cl % 2:
             act("et%d" % cl, T.ET[:, 128 * cl:128 * cl + 128], T.BO[:], F.Identity, ["BO", "LM"], ["ET%d" % cl], 128, scale=T.LM[:, cl:cl + 1])
@@ -159,163 +166,169 @@ def build(g, T, topo, core):
     vts("ck1", T.CK[0:32, :], T.IR[0:32, :], 8.0, 64.0, A.add, A.mult, ["IR"], ["CK"], 128)
     vset("ck2", T.CK[32:64, :], -524288.0, ["CK"], 64)
     vts("rs", T.RS[:], T.IR[:], 0.0, 67108864.0, A.is_equal, A.mult, ["IR"], ["RS"], 128)
-    vts("cc2", T.CC[:], T.CC[:], LANE, None, A.add, None, ["CC", "C01"], ["CC"], 16)
-    act("if", T.IF[:], ID, F.Identity, ["IW"], ["IF"], 128)
     vset("sg0", T.SG[:], -1.0, ["SG"], 128)
     vset("yg0", T.YG[:], -1.0, ["YG"], 128)
-    vset("sw0", T.SW[:], -0.5, ["SW"], 16)
+    vset("sw0", T.SW[:], 0.5, ["SW"], 16)
     vset("hh0", T.HH[:], -64.0, ["HH"], 16)
     pool("sw_e", lambda: g.affine_select(T.XW0[:, 0:2048:2], T.CU[:, 2049:4096:2], [[0, 1024]], A.is_gt, 0.0, 1, 0), ["CUb"], ["SWe"], 1024)
     pool("sw_o", lambda: g.affine_select(T.XW0[:, 1:2048:2], T.CU[:, 2048:4096:2], [[0, 1024]], A.is_gt, 0.0, 1, 0), ["CUb"], ["SWo"], 1024)
-    dma("c_sw", "sync", T.XW1[:, 0:2048], T.XW0[:, 0:2048], ["SWe", "SWo"], ["SW1"], 524288)
+    dma("c_sw", "sync", T.XW1[:, 0:2048], T.XW0[:, 0:2048], ["SWe", "SWo", "q4"], ["SW1", "q5"], 524288)
+    dma("l_gap", "sync", T.TB[:, 4096:6144], T.spare[:], ["q5"], ["gap"], 1048576)
     SWK = [["SWe", "SWo"], ["SW1"]]
-    pool("spf", lambda: g.affine_select(T.TB[:, 0:2048], T.SI[:], [[0, 2048]], A.is_gt, 0.0, 1, 0), ["SI"], ["spare"], 2048)
-    dma("c_gap", "sync", T.TB[:, 8192:10240], T.TB[:, 0:2048], ["spare"], ["gap"], 1048576)
 
-    def turn(out, mats, y, hf, names, hi=16, stop=False):
-        lst = []
-        for gw in range(2):
-            for gr in range(2):
-                j = 2 * gw + gr
-                lst.append((out[:, gr:8:2, 0:hi], mats[:, 128 * j:128 * j + 128], y[:, 8 * hf + gw:8 * hf + 8:2, 0:hi], False, False, 4 * hi))
-        return lst
+    def turn(out, mats, y, hf, stop=False):
+        return [(out[:, 64 * (j % 2):64 * (j % 2) + 64], mats[:, 128 * j:128 * j + 128], y[:, 8 * hf + j // 2:8 * hf + 8:2, :], False, stop and j == 3, 64) for j in range(4)]
+
+    def state(t, hf):
+        c0 = 128 * hf
+        return (T.HL[:, 256 * t + c0:256 * t + c0 + 128], "h%d_%d" % (t, hf),
+                T.AH[:, 256 * (t % 2) + c0:256 * (t % 2) + c0 + 128], "a%d_%d" % (t % 2, hf))
+
+    def blocks(name, b0, n):
+        return ["%s_%d" % (name, b) for b in range(b0 // 16, (b0 + n) // 16)]
 
     def pre(t, hf):
-        c0 = 128 * hf
-        h = T.HL[:, 256 * t + c0:256 * t + c0 + 128]; hk = "h%d_%d" % (t, hf)
-        a = T.AH[:, 256 * (t % 2) + c0:256 * (t % 2) + c0 + 128]; ak = "a%d_%d" % (t % 2, hf)
-        u = "%d_%d" % (t, hf)
-        b1 = ("X1", "v" + u); ts = slice(8 * hf, 8 * hf + 8)
-        mm("v1" + u, [(T.X1[:, 0:128], T.IDH[:], a, True, False, 128), (T.X1[:, 0:128], T.WB[:], h, False, True, 128)], [hk, ak, "WB", "IDH"], [], b1)
-        act("rr" + u, T.RR[:, c0:c0 + 128], T.X1[:, 0:128], F.Identity, [], ["RR%d" % hf], 128, b1, bias=524288.0)
-        bh = ("H4%d" % hf, u); v2 = H4[hf][:, 128:256]
-        mm("v2" + u, [(H4[hf][:, 0:128], ID, h, True, True, 128), (v2, T.IDH[:], a, True, False, 128), (v2, T.WB[:], h, False, False, 128)], [hk, ak, "WB", "IDH", "IW"], [], bh)
-        mm("v3" + u, [(v2, T.NI[:], T.RR[:, c0:c0 + 128], False, True, 128)], ["RR%d" % hf, "NI"], [], bh)
-        vts("at" + u, T.AT[:, c0:c0 + 128], v2, 526336.0, None, A.add, None, [], ["AT%d" % hf], 128, bh)
-        op("ya" + u, "dve", lambda: V.transpose(T.YA[:, 8 * hf:8 * hf + 8, :], a), [ak], ["YA%d" % hf], "el", 64)
+        c0 = 128 * hf; u = "%d_%d" % (t, hf); f = "%d" % hf
+        h, hk, a, ak = state(t, hf)
+        b1, b2, bh = ("K" + f, "v" + u), ("P" + f, "v" + u), ("H" + f, "h" + u)
+        v1, v2 = KB[hf][:, 0:128], PB[hf][:, 0:128]
+        mm("va" + u, [(v1, T.IDH[:], a, True, False, 128)], [ak, "IDH"], [], b1)
+        mm("vb" + u, [(v2, T.IDH[:], a, True, False, 128)], [ak, "IDH"], [], b2)
+        mm("v1" + u, [(v1, T.WB[:], h, False, True, 128)], [hk, "WB"], [], b1)
+        mm("v2" + u, [(v2, T.WB[:], h, False, False, 128)], [hk, "WB"], [], b2)
+        if OPT["rr"] == "act":
+            act("rr" + u, T.RR[:, c0:c0 + 128], v1, F.Identity, [], ["RR" + f], 128, b1, bias=524288.5)
+        else:
+            vts("rr" + u, T.RR[:, c0:c0 + 128], v1, 524288.5, None, A.add, None, [], ["RR" + f], 128, b1)
+        mm("v3" + u, [(v2, T.NI[:], T.RR[:, c0:c0 + 128], False, True, 128)], ["RR" + f, "NI"], [], b2)
+        for e in range(2):
+            vts("at" + u + "_%d" % e, T.AT[:, c0 + 64 * e:c0 + 64 * e + 64], PB[hf][:, 64 * e:64 * e + 64], 526336.0, None, A.add, None, [], blocks("AT" + f, 64 * e, 64), 64, b2)
+        mm("h4" + u, [(HB[hf][:, :, r], ID, h, True, True, 128) for r in range(4)], [hk, "IW"], [], bh, 2)
+        vtr("ya" + u, T.YA[:, 8 * hf:8 * hf + 8, :], a, [ak], ["YA" + f], 64)
 
     def heavy(t, hf):
-        c0 = 128 * hf
-        u = "%d_%d" % (t, hf)
-        h = T.HL[:, 256 * t + c0:256 * t + c0 + 128]; hk = "h%d_%d" % (t, hf)
-        X, M, Pm = XW[hf], MX[hf], PP[hf]
-        bh = ("H4%d" % hf, u); bp = ("PP%d" % hf, u)
-        mm("p0" + u, [(Pm[:, 0:128], T.BM2[:], h, True, False, 128)], ["BM2", hk], [], bp)
-        for q in range(NQ):
-            xk = ["x%d_%d_%d" % (hf, q, e) for e in range(NG_)]; w = u + "_%d" % q
-            cq = slice(CA * q, CA * q + CA); x0 = 2048 + 16 * CA * q
-            for e in range(NG_):
-                n = CA // NG_; b0 = CA * q + n * e
-                act("gg" + w + "_%d" % e, X[:, 2048 + 16 * b0:2048 + 16 * (b0 + n)], T.CU[:].indirect(T.AT[:, c0 + b0:c0 + b0 + n]), F.Copy,
-                    ["CUa", "CUb", "AT%d" % hf], [xk[e]], 16 * n, kind="gat")
-            mm("px" + w, [(Pm[:, cq], T.EM2[:, 15 - i:143 - i], X[:, x0 + i:x0 + 16 * CA:16], False, False, CA) for i in range(16)], xk + ["EM2", "EM2z"], [], bp)
-            for j in range(0, 16, 4):
-                for i in range(j, j + 4):
-                    vtt("mx" + w + "_%d" % i, M[:, 128 * i + CA * q:128 * i + CA * q + CA], X[:, x0 + i:x0 + 16 * CA:16], H4[hf][:, cq], A.max, xk, ["m%d_%d_%d" % (hf, q, i)], CA, bh)
-                mm("pm" + w + "_%d" % j, [(Pm[:, cq], T.E4[:, 15 - i:143 - i], M[:, 128 * i + CA * q:128 * i + CA * q + CA], False, q == NQ - 1 and i == 15, CA) for i in range(j, j + 4)],
-                   ["m%d_%d_%d" % (hf, q, i) for i in range(j, j + 4)] + ["E4", "E4z"], [], bp)
+        c0 = 128 * hf; u = "%d_%d" % (t, hf); f = "%d" % hf
+        h, hk, a, ak = state(t, hf)
+        X, M, D = XW[hf], MX[hf], PB[hf]
+        bh, bp = ("H" + f, "h" + u), ("P" + f, "d" + u)
+        mm("p0" + u, [(D[:, 0:128], T.BM2[:], h, True, False, 128)], ["BM2", hk], [], bp)
+        for b0, n in cuts(OPT["gat"]):
+            act("gg" + u + "_%d" % b0, X[:, 2048 + 16 * b0:2048 + 16 * (b0 + n)], T.CU[:].indirect(T.AT[:, c0 + b0:c0 + b0 + n]), F.Copy,
+                ["CUa", "CUb"] + blocks("AT" + f, b0, n), blocks("x" + f, b0, n), 16 * n, kind="gat")
+        for b0, n in cuts(OPT["pm"]):
+            mm("px" + u + "_%d" % b0, [(D[:, b0:b0 + n], T.EM2[:, 15 - i:143 - i], X[:, 2048 + 16 * b0 + i:2048 + 16 * (b0 + n):16], False, False, n) for i in range(16)],
+               blocks("x" + f, b0, n) + ["EM2", "EM2z"], [], bp)
+        for b0, n in cuts(OPT["mx"]):
+            for j in range(4):
+                vtt("mx" + u + "_%d_%d" % (b0, j), M[:, 512 * j + 4 * b0:512 * j + 4 * (b0 + n)], X[:, 2048 + 16 * b0 + j:2048 + 16 * (b0 + n):4], HB[hf][:, b0:b0 + n, :], A.max,
+                    blocks("x" + f, b0, n), blocks("m%d_%d" % (hf, j), b0, n), 4 * n, bh)
+        for b0, n in cuts(OPT["pm"]):
+            for j in range(4):
+                mm("pm" + u + "_%d_%d" % (b0, j), [(D[:, b0:b0 + n], T.E4[:, 15 - i:143 - i], M[:, 512 * j + 4 * b0 + i // 4:512 * j + 4 * (b0 + n):4], False, b0 + n == 128 and i == 15, n) for i in range(j, 16, 4)],
+                   blocks("m%d_%d" % (hf, j), b0, n) + ["E4", "E4z"], [], bp)
+
+    def notes(u, hs, win, wk, a, ak):
+        ts = slice(8 * hs[0], 8 * hs[-1] + 8); n = 8 * len(hs); f = ["%d" % hf for hf in hs]
+        vts("zb" + u, T.ZB[:, ts], T.LL[:, hs[0]:hs[-1] + 1, 3, :], 0x1700, None, A.bitwise_and, None, ["Z" + e for e in f], ["ZB" + e for e in f], n)
+        vtt("zc" + u, T.ZC[:, ts], T.ZB[:, ts], T.CC[:, ts], A.add, ["ZB" + e for e in f] + ["CC"], ["ZC" + e for e in f], n)
+        vcp("ls" + u, T.LS[:, ts], T.ZC[:, ts], ["ZC" + e for e in f], ["LS" + e for e in f], n)
+        vcp("sc" + u, win.indirect(T.LS[:, ts]), a, ["LS" + e for e in f] + ak, wk, 16 * n, kind="sca")
 
     def post(t, hf):
         c0 = 128 * hf; cs = slice(c0, c0 + 128); ts = slice(8 * hf, 8 * hf + 8)
         u = "%d_%d" % (t, hf); f = "%d" % hf
-        h = T.HL[:, 256 * t + c0:256 * t + c0 + 128]; hk = "h%d_%d" % (t, hf)
-        a = T.AH[:, 256 * (t % 2) + c0:256 * (t % 2) + c0 + 128]; ak = "a%d_%d" % (t % 2, hf)
-        bp = ("PP%d" % hf, u); bk = ("KP", u); br = ("RP", u); bs = ("X1", "s" + u)
-        Pm = PP[hf]; K = T.KP[:, 0:128]
-        if FAR_ACT:
-            act("far" + u, T.FAR[:, cs], Pm[:, 0:128], F.Relu, ["THR"], ["FAR" + f], 128, bp, scale=1024.0, bias=THR)
-        else:
-            vts("far" + u, T.FAR[:, cs], Pm[:, 0:128], THR, 1024.0, A.is_gt, A.mult, ["THR"], ["FAR" + f], 128, bp)
+        h, hk, a, ak = state(t, hf)
+        bp, bk, br, bs, bq = ("P" + f, "d" + u), ("K" + f, "k" + u), ("P" + f, "r" + u), ("K" + f, "s" + u), ("H" + f, "q" + u)
+        D, K, R = PB[hf][:, 0:128], KB[hf][:, 0:128], PB[hf]
+        mm("o0" + u, [(K, T.ONE[:], T.CK[:], True, False, 128)], ["ONE", "CK"], [], bk)
+        mm("o1" + u, turn(KB[hf], T.SA, T.YA, hf), ["YA" + f, "SA0", "SA1", "SA2", "SA3"], [], bk)
+        mm("o2" + u, turn(KB[hf], T.SS, T.YG, hf), ["YG", "SS0", "SS1", "SS2", "SS3"], [], bk)
+        vts("far" + u, T.FAR[:, cs], D, THR, 1024.0, A.is_gt, A.mult, ["THR"], ["FAR" + f], 128, bp)
+        vtt("dz" + u, T.DZ[:, cs], D, T.FAR[:, cs], A.min, ["FAR" + f], ["DZ" + f], 128, bp)
+        vtr("yd" + u, T.YD[:, ts, :], T.DZ[:, cs], ["DZ" + f], ["YD" + f], 64)
+        mm("k1" + u, turn(KB[hf], T.SD, T.YD, hf, True), ["YD" + f, "SD0", "SD1", "SD2", "SD3"], [], bk)
         for e in range(2):
-            vtt("dz" + u + "_%d" % e, T.DZ[:, 8 * hf + e:8 * hf + 8:2, :], Pm[:, 64 * e:64 * e + 64], T.FAR[:, c0 + 64 * e:c0 + 64 * e + 64], A.min, ["FAR" + f], ["DZ%d" % e + f], 64, bp)
-        op("yd" + u, "dve", lambda: V.transpose(T.YD[:, ts, :], T.DZ[:, ts, :]), ["DZ0" + f, "DZ1" + f], ["YD" + f], "el", 64)
-        bo = ("X2", "o" + u)
-        lst = [(T.X2[:, 0:8, :], T.ONE[:, 0:128], T.CK[:], True, False, 128)] + turn(T.X2, T.SS, T.YG, hf, None) + turn(T.X2, T.SA, T.YA, hf, None)
-        lst[-1] = lst[-1][0:4] + (True, lst[-1][5])
-        mm("o0" + u, lst, ["ONE", "CK", "YG", "YA" + f, "SS0", "SS1", "SS2", "SS3", "SA0", "SA1", "SA2", "SA3"], [], bo)
-        act("os" + u, T.OS[:, cs], T.X2[:, 0:8, :], F.Identity, [], ["OS" + f], 128, bo)
-        mm("k0" + u, [(K, T.IF[:], T.OS[:, cs], True, False, 512)], ["IF", "OS" + f], [], bk)
-        mm("k1" + u, [(T.KP[:, 64 * (j % 2):64 * (j % 2) + 64], T.SD[:, 128 * j:128 * j + 128], T.YD[:, 8 * hf + j // 2:8 * hf + 8:2, :], False, j == 3, 64) for j in range(4)],
-           ["YD" + f, "SD0", "SD1", "SD2", "SD3"], [], bk)
-        op("scan" + u, "dve", lambda: V.tensor_tensor_scan(T.KS[:, cs], T.RS[:], K, 0.0, A.add, A.min), ["RS"], ["KS" + f], "el", 128, bk)
-        km = T.KS[:, c0 + 15:c0 + 128:16]
-        N_, LP, Z = T.LL[:, hf, 0:8], T.LL[:, hf, 8:16], T.LL[:, hf, 16:24]
-        U, NG = T.RQ[:, hf, 0:8], T.RQ[:, hf, 8:16]
-        vcp("ki" + u, T.KI[:, ts], km, ["KS" + f], ["KI" + f], 8)
-        vts("ng" + u, NG, km, -16711680.0, 8192.0, A.is_ge, A.mult, ["KS" + f], ["NG" + f], 8)
-        vts("n" + u, N_, T.KI[:, ts], 2047, None, A.bitwise_and, None, ["KI" + f], ["N" + f], 8)
-        vts("o" + u, T.OO[:, ts], T.KI[:, ts], 11, 31, A.logical_shift_right, A.bitwise_and, ["KI" + f], ["OO" + f], 8)
-        vtt("z" + u, Z, N_, NG, A.add, ["N" + f, "NG" + f], ["Z" + f], 8)
-        vts("kk" + u, T.KK[:, ts], T.KI[:, ts], 11, 15, A.logical_shift_right, A.bitwise_and, ["KI" + f], ["KK" + f], 8)
-        vtt("x" + u, T.XX[:, ts], T.KK[:, ts], T.CX[:], A.add, ["KK" + f, "CX"], ["XX" + f], 8)
-        vtt("lp" + u, LP, T.XX[:, ts], Z, A.min, ["XX" + f, "Z" + f], ["LP" + f], 8)
+            op("scan" + u + "_%d" % e, "dve", lambda e=e: V.tensor_tensor_scan(T.KS[:, 64 * hf:64 * hf + 64, e], T.RS[:, 0:64], KB[hf][:, 64 * e:64 * e + 64], 0.0, A.add, A.min),
+               ["RS"], ["KS%d" % e + f], "el", 64, bk)
+        km = T.KS[:, 64 * hf + 15:64 * hf + 64:16, :]
+        L, Q = T.LL, T.RQ
+        vcp("ki" + u, T.KI[:, ts], km, ["KS0" + f, "KS1" + f], ["KI" + f], 8)
+        vts("ng" + u, Q[:, hf, 2, :], km, -16711680.0, 4096.0, A.is_ge, A.mult, ["KS0" + f, "KS1" + f], ["NG" + f], 8)
+        vts("kk" + u, L[:, hf, 1, :], T.KI[:, ts], 11, 15, A.logical_shift_right, A.bitwise_and, ["KI" + f], ["KK" + f], 8)
+        vts("nn" + u, L[:, hf, 0, :], T.KI[:, ts], 2047, None, A.bitwise_and, None, ["KI" + f], ["N" + f], 8)
+        vts("oo" + u, L[:, hf, 2, :], T.KI[:, ts], 11, 31, A.logical_shift_right, A.bitwise_and, ["KI" + f], ["OO" + f], 8)
+        vtt("zx" + u, L[:, hf, 3:5, :], L[:, hf, 0:2, :], Q[:, hf, 2:4, :], A.add, ["N" + f, "KK" + f, "NG" + f, "CX" + f], ["Z" + f, "LP" + f], 16)
+        vtt("lp" + u, L[:, hf, 4, :], L[:, hf, 4, :], L[:, hf, 3, :], A.min, ["LP" + f, "Z" + f], ["LP" + f], 8)
         lu = T.LU[:, 16 * hf:16 * hf + 16]
+        lt_, lsp = T.LU[:, 16 * hf:16 * hf + 8], T.LU[:, 16 * hf + 8:16 * hf + 16]
         if t == 0:
-            vcp("lu" + u, lu, T.LL[:, hf, 0:16], ["N" + f, "LP" + f], ["LU" + f], 16)
-            lt_, lsp = T.LU[:, 16 * hf:16 * hf + 8], T.LU[:, 16 * hf + 8:16 * hf + 16]
+            vcp("lu" + u, lu, L[:, hf, 0:5:4, :], ["N" + f, "LP" + f], ["LU" + f], 16)
             win, wk = T.TB[:, 0:2048], ["spare"]
         else:
-            vcp("lu" + u, lu, T.LL[:, hf, 8:24], ["Z" + f, "LP" + f], ["LU" + f], 16)
-            lsp, lt_ = T.LU[:, 16 * hf:16 * hf + 8], T.LU[:, 16 * hf + 8:16 * hf + 16]
-            win, wk = T.TB[:, 0:10240], ["spare", "gap"]
-        vtt("d" + u, T.DD[:, ts], NG, T.SW[:, ts], A.mult, ["NG" + f, "SW"], ["DD" + f], 8)
-        vtt("u" + u, U, T.OO[:, ts], T.DD[:, ts], A.add, ["OO" + f, "DD" + f], ["U" + f], 8)
-        mm("r0" + u, [(T.RP[:, 0:256], T.DG[:], T.ONE[:], True, False, 256), (T.RP[:, 0:128], T.I32K[:], T.SG[:, cs], False, False, 128),
-                      (T.RP[:, 128:256], ID, h, False, False, 128)], ["DG", "ONE", "ONEz", "I32K", "SG", "IW", hk], [], br)
-        mm("r1" + u, [(T.RP[:, cl:256:16], T.ET[:, 128 * cl:128 * cl + 128], T.RQ[:, hf, :], False, cl == 15, 16) for cl in range(16)], ETK + ["U" + f, "NG" + f], [], br)
-        act("hm" + u, T.HM[:, cs], T.RP[:, 128:256], F.Relu, [], ["HM" + f], 128, br)
-        act("p1" + u, T.P1[:, cs], T.RP[:, 0:128], F.Relu, [], ["P1" + f], 128, br, scale=-1.0)
-        vtt("t2" + u, T.T2[:, cs], a, T.RP[:, 0:128], A.min, [ak], ["T2" + f], 128, br)
-        act("xu" + u, T.XU[:, cs], XW[hf][:].indirect(lsp), F.Copy, SWK[hf] + ["x%d_%d_%d" % (hf, q, e) for q in range(NQ) for e in range(NG_)] + ["LU" + f], ["XU" + f], 128, kind="gat")
-        mm("s" + u, [(T.X1[:, 0:128], ID, T.XU[:, cs], True, False, 128), (T.X1[:, 0:128], T.NI[:], h, False, False, 128),
-                     (T.X1[:, 0:128], ID, T.HM[:, cs], False, True, 128)], ["XU" + f, "HM" + f, hk, "IW", "NI"], [], bs)
+            vcp("lu" + u, lu, L[:, hf, 3:5, :], ["Z" + f, "LP" + f], ["LU" + f], 16)
+            win, wk = T.TB[:, 0:6144], ["spare", "gap"]
+        vtt("ee" + u, Q[:, hf, 4, :], Q[:, hf, 2, :], T.SW[:, ts], A.mult, ["NG" + f, "SW"], ["EE" + f], 8)
+        vtt("ju" + u, Q[:, hf, 0:2, :], L[:, hf, 1:3, :], Q[:, hf, 2:5:2, :], A.subtract, ["KK" + f, "OO" + f, "NG" + f, "EE" + f], ["J" + f, "U" + f], 16)
+        mm("r0" + u, [(R[:, 0:128], T.I8[:], T.SG[:, cs], True, False, 128)], ["I8", "SG"], [], br)
+        mm("r1" + u, [(R[:, cl:128:16], T.ET[:, 128 * cl:128 * cl + 128], Q[:, hf, 1, :], False, cl == 15, 8) for cl in range(16)], ETK + ["U" + f], [], br)
+        bm = ("H" + f, "m" + u); hp = HB[hf][:, 32:64, :]
+        mm("h0" + u, [(hp, ID, h, True, False, 128)], ["IW", hk], [], bm)
+        mm("h1" + u, [(hp, T.BO[:], T.FAR[:, cs], False, True, 128)], ["BO", "FAR" + f], [], bm)
+        act("hm" + u, T.HM[:, cs], hp, F.Relu, [], ["HM" + f], 128, bm, bias=-16384.0)
+        act("p1" + u, T.P1[:, cs], R[:, 0:128], F.Relu, ["C3"], ["P1" + f], 128, br, scale=-4096.0, bias=T.COL[:, 3:4])
         sp = T.SP[:, 256 * t + c0:256 * t + c0 + 128]
-        act("sp" + u, sp, T.X1[:, 0:128], F.Abs, [], ["sp" + u], 128, bs)
+        xk = SWK[hf] + blocks("x" + f, 0, 128) + ["LU" + f]
+        if OPT["speech"] == "dve":
+            vtt("xu" + u, T.XU[:, cs], XW[hf][:].indirect(lsp), T.HM[:, cs], A.subtract, xk + ["HM" + f], ["XU" + f], 128, kind="gat")
+            act("sp" + u, sp, T.XU[:, cs], F.Abs, ["XU" + f], ["sp" + u], 128)
+        else:
+            act("xu" + u, T.XU[:, cs], XW[hf][:].indirect(lsp), F.Copy, xk, ["XU" + f], 128, kind="gat")
+            mm("s" + u, [(K, ID, T.XU[:, cs], True, False, 128), (K, T.NI[:], T.HM[:, cs], False, True, 128)], ["XU" + f, "HM" + f, "IW", "NI"], [], bs)
+            act("sp" + u, sp, K, F.Abs, [], ["sp" + u], 128, bs)
         dst = T.cores[(rank + 1 + t % (ranks - 1)) % ranks]
         rid, pid, _ = topo.addr(dst); mask = topo.mask(core, dst); ne = len(topo.engines(core, dst))
         land = T.HL[:, 256 * (t + 1) + c0:256 * (t + 1) + c0 + 128]
         op("send" + u, "pool", lambda: g.remote_dma(land, sp, T.sem["ar" + u], T.sem.sent, pid, rid, mask), ["sp" + u], ["snd" + u], "send", ne)
         op("ar" + u, "net", None, ["snd" + u], ["h%d_%d" % (t + 1, hf)], "arr", ne)
         vtt("t1" + u, T.T1[:, cs], win.indirect(lt_), T.P1[:, cs], A.min, wk + ["LU" + f, "P1" + f], ["T1" + f], 128, kind="gat")
+        q = HB[hf][:, 0:32, :]
+        mm("q" + u, [(q, T.IDH[:], a, True, False, 128), (q, T.NI[:], T.P1[:, cs], False, True, 128)], [ak, "IDH", "NI", "P1" + f], [], bq)
         if t < STEPS - 1:
-            na = T.AH[:, 256 * ((t + 1) % 2) + c0:256 * ((t + 1) % 2) + c0 + 128]
-            vtt("an" + u, na, T.T1[:, cs], T.T2[:, cs], A.max, ["T1" + f, "T2" + f], ["a%d_%d" % ((t + 1) % 2, hf)], 128, kind="tt")
+            _, _, na, nk = state(t + 1, hf)
+            vtt("an" + u, na, T.T1[:, cs], q, A.max, ["T1" + f], [nk], 128, bq)
         else:
-            vtt("an" + u, T.YS[:, cs], T.T1[:, cs], T.T2[:, cs], A.max, ["T1" + f, "T2" + f], ["YS" + f], 128, kind="tt")
+            vtt("an" + u, T.YS[:, cs], T.T1[:, cs], q, A.max, ["T1" + f], ["YS" + f], 128, bq)
             dma("o_s" + f, "sync", T.ys[:, cs], T.YS[:, cs], ["YS" + f], ["ys" + f], 65536)
             dma("o_h" + f, "sync", T.yh[:, cs], land, ["h%d_%d" % (t + 1, hf)], ["yh" + f], 32768)
+            notes(u, [hf], T.GO[:], ["go%d" % j for j in range(OPT["conv"])], a, [ak])
 
     def both(t):
         u = "%d" % t
-        vts("zb" + u, T.ZB[:], T.LL[:, :, 16:24], 0x2700, None, A.bitwise_and, None, ["Z0", "Z1"], ["ZB"], 16)
-        vtt("zc" + u, T.ZC[:], T.ZB[:], T.CC[:], A.add, ["ZB", "CC"], ["ZC"], 16)
-        vcp("ls" + u, T.LS[:], T.ZC[:], ["ZC"], ["LS"], 16)
-        a = T.AH[:, 256 * (t % 2):256 * (t % 2) + 256]
-        vcp("sc" + u, T.TB[:, 8192:18432].indirect(T.LS[:]), a, ["LS", "a%d_0" % (t % 2), "a%d_1" % (t % 2)], ["gap"], 256, kind="sca")
         if t == STEPS - 1:
-            dma("o_g", "sync", T.yg[:], T.TB[:, 8192:10240], ["gap"], ["yg"], 1048576)
+            dma("o_g", "act", T.yg[:], T.GO[:, 0:2048], ["go%d" % j for j in range(OPT["conv"])], ["yg"], 1048576)
             return
-        NG = T.RQ[:, :, 8:16]
+        notes(u, [0, 1], T.TB[:, 4096:10240], ["gap"], T.AH[:, 256 * (t % 2):256 * (t % 2) + 256], ["a%d_0" % (t % 2), "a%d_1" % (t % 2)])
+        if t == STEPS - 2:
+            n = 2048 // OPT["conv"]
+            for j in range(OPT["conv"]):
+                pool("cv%d" % j, lambda j=j: g.affine_select(T.GO[:, n * j:n * j + n], T.TB[:, 4096 + n * j:4096 + n * j + n], [[0, n]], A.is_gt, 0.0, 1, 0), ["gap"], ["go%d" % j], n)
+        NG, EE = T.RQ[:, :, 2, :], T.RQ[:, :, 4, :]
         bm = ("X2", "m" + u); bh = ("X2", "h" + u)
         mm("mc" + u, [(T.X2[:, 0, :], T.OM[:], NG, True, True, 16)], ["OM", "NG0", "NG1"], [], bm)
-        act("ma" + u, T.MC[:, 0:16], T.X2[:, 0, :], F.Identity, [], ["MC"], 16, bm, scale=FS, bias=255.0625 * FS, accum_out=T.MC[:, 16:17])
-        vts("mr" + u, T.MC[:, 17:18], T.MC[:, 16:17], 402653184.0 * abs(FS), 402653184.0 * abs(FS), A.add, A.subtract, ["MC"], ["MR"], 1)
+        act("ma" + u, T.MC[:, 0:16], T.X2[:, 0, :], F.Identity, [], ["MC"], 200, bm, bias=255.0625, accum_out=T.MC[:, 16:17])
+        vts("mr" + u, T.MC[:, 17:18], T.MC[:, 16:17], 402653184.0, 402653184.0, A.add, A.subtract, ["MC"], ["MR"], 1)
         vts("thr" + u, THR, T.MC[:, 16:17], T.MC[:, 17:18], T.WF[:, 4:5], A.subtract, A.add, ["WFt", "MC", "MR"], ["THR"], 1)
-        vts("sw" + u, T.SW[:], T.DD[:], -1.0, 0.5, A.is_lt, A.subtract, ["DD0", "DD1"], ["SW"], 16)
-        vts("wn" + u, T.WN[:], T.DD[:], -1.0, 4096.0, A.is_ge, A.mult, ["DD0", "DD1"], ["WN"], 16)
-        vtt("j" + u, T.JJ[:], T.KK[:], NG, A.subtract, ["KK0", "KK1", "NG0", "NG1"], ["JJ"], 16)
-        vtt("tt" + u, T.TT[:], T.HH[:], T.WN[:], A.subtract, ["HH", "WN"], ["TT"], 16)
-        vtt("hh" + u, T.HH[:], T.JJ[:], T.TT[:], A.max, ["JJ", "TT"], ["HH"], 16)
+        vts("sw" + u, T.SW[:], EE, 1.0, 0.5, A.is_le, A.subtract, ["EE0", "EE1"], ["SW"], 16)
+        vtt("tt" + u, T.TT[:], T.HH[:], EE, A.min, ["HH", "EE0", "EE1"], ["TT"], 16)
+        vtt("hh" + u, T.HH[:], T.RQ[:, :, 0, :], T.TT[:], A.max, ["J0", "J1", "TT"], ["HH"], 16)
         mm("hr" + u, [(T.X2[:, 0:16, cl], T.ET[:, 128 * cl:128 * cl + 128], T.HH[:], True, True, 16) for cl in range(16)], ETK + ["HH"], [], bh)
-        act("sg" + u, T.SG[:], T.X2[:, 0:16, :], F.Sign, ["C4"], ["SG"], 256, bh, scale=-1.0 / 4096.0, bias=T.COL[:, 4:5])
-        op("yg" + u, "dve", lambda: V.transpose(T.YG[:], T.SG[:]), ["SG"], ["YG"], "el", 128)
+        act("sg" + u, T.SG[:], T.X2[:, 0:16, :], F.Sign, ["C4"], ["SG"], 256, bh, scale=-1.0, bias=T.COL[:, 4:5])
+        vtr("yg" + u, T.YG[:], T.SG[:], ["SG"], ["YG"], 128)
 
     for t in range(STEPS):
-        for part in (("pre", pre), ("heavy", heavy), ("post", post)):
+        for part in (pre, heavy, post):
             for hf in range(2):
-                tag[0] = part[0] + str(hf)
-                part[1](t, hf)
-        tag[0] = "both"
+                part(t, hf)
         both(t)
     return ops
 
@@ -326,8 +339,6 @@ def cost(o, c):
         return 10.0 + n * c["pe"]
     if k == "el":
         return c["fix"] + max(n, 64) * c["cyc"]
-    if k == "tt":
-        return c["fix"] + n * c["tt"] * c["cyc"]
     if k == "gat":
         return 60.0 + n * c["gat"] * c["cyc"]
     if k == "sca":
@@ -337,11 +348,8 @@ def cost(o, c):
     if k == "dma":
         return 60.0
     if k == "send":
-        return 300.0
+        return c["send"]
     return 0.0
-
-
-ORDERED = ("KP", "RP", "H40", "H41", "PP0", "PP1")
 
 
 def depend(ops):
@@ -364,23 +372,13 @@ def depend(ops):
         if b is not None:
             if b in sess:
                 d.update(j for j in sess[b] if j == sess[b][0] or o["stop"] or ops[j]["eng"] != o["eng"])
-            elif b[0] in ORDERED and b[0] in lastof:
+            elif b[0] in lastof:
                 d.update(sess[lastof[b[0]]])
             sess.setdefault(b, []).append(i)
             lastof[b[0]] = b
         d.discard(i)
         o["dep"] = d
-    return sess
-
-
-def finish(o, start, c, dmafree):
-    if o["kind"] == "dma":
-        s = max(start + c["dma"] * 0.6, dmafree[0])
-        dmafree[0] = s + o["n"] / c["bw"]
-        return dmafree[0] + c["dma"] * 0.4
-    if o["kind"] == "arr":
-        return start + c["rem"]
-    return start + cost(o, c)
+        o["hard"] = [j for j in d if not soft(o, ops[j])]
 
 
 def soft(o, p):
@@ -388,77 +386,106 @@ def soft(o, p):
         return False
     if o["eng"] == "pe":
         return True
+    shared = (set(o["r"]) & set(p["w"])) | (set(o["w"]) & set(p["r"])) | (set(o["w"]) & set(p["w"]))
+    if o["kind"] == "dma" and p["kind"] == "dma":
+        return all(k[0] == "q" for k in shared)
     if o["bank"] is not None and p["bank"] is not None and o["bank"][0] == p["bank"][0]:
-        return not (set(o["r"]) & set(p["w"]) or set(o["w"]) & set(p["r"]) or set(o["w"]) & set(p["w"]))
+        return not shared
     return False
 
 
 def ready_at(ops, o, end, free, c):
     s = free.get(o["eng"], 0.0)
-    for j in o["dep"]:
-        p = ops[j]
-        if soft(o, p):
-            continue
-        s = max(s, end[j] + (c["own"] if p["eng"] == o["eng"] else c["lat"]))
+    for j in o["hard"]:
+        s = max(s, end[j] + (c["own"] if ops[j]["eng"] == o["eng"] else c["lat"]))
     return s
 
 
-TUNE = {'slack': 30.0, 'lam': 20, 'l_h': 200000.0, 'l_a': 100000.0, 'pre0': 4700.0, 'post0': 3100.0, 'both': 600.0, 'heavy1': -1800.0, 'rr:pre0': 2000.0, 'o_:post1': 800.0, 'lu:post0': -2400.0, 'hh:both': -1000.0, 'v1:pre0': 6300.0, 'p0:heavy0': -2200.0, 'mc:both': -2200.0, 'sp:post1': 1300.0, 'sc:post1': -1000.0, 'pm:heavy0': -1000.0, 'px:heavy0': 1700.0, 'yd:post0': 400.0, 'xu:post0': 6000.0, 'sp:post0': 4100.0, 'ar:post0': 9100.0, 'p1:post1': 900.0, 'v2:pre0': -1300.0, 'ls:both': -3700.0, 'k0:post1': -200.0, 'k0:post0': -200.0, 'an:post0': 3000.0, 'o_:post0': -7200.0, 'dz:post0': 1500.0, 'rr:pre1': -20000.0, 'pre1': 13400.0, 'lp:post1': -1500.0, 't2:post0': 8700.0, 'at:pre1': -400.0, 'pm:heavy1': -5600.0, 'sw:both': 300.0, 'v3:pre0': 14300.0, 'yg:both': 5000.0, 'ma:both': 600.0, 'p0:heavy1': -1100.0, 'k1:post1': 2300.0, 'lp:post0': 3800.0, 'se:post0': 6200.0, 'ar:post1': -6300.0, 'v2:pre1': -600.0, 'mx:heavy0': -2400.0, 'fa:post1': 6500.0, 'lu:post1': -3700.0, 'wn:both': 900.0, 'kk:post1': -2400.0, 'mr:both': -500.0, 'sg:both': -400.0, 'r1:post0': -1100.0, 'hr:both': 7600.0, 'fa:post0': -2100.0, 'ng:post1': -600.0, 'v3:pre1': 400.0, 'sc:post0': 4700.0, 'r1:post1': -2600.0, 'r0:post1': 10400.0, 'os:post1': -2500.0, 't1:post1': -300.0, 'ya:pre1': -2200.0, 'ki:post0': -1300.0, 'dz:post1': 600.0, 'zc:both': 1000.0, 'zb:both': -900.0, 't1:post0': 1200.0, 'heavy0': -700.0, 'ng:post0': -1200.0, 'k1:post0': 4300.0, 'ki:post1': -1900.0, 'mx:heavy1': -400.0, 'kk:post0': 300.0, 'th:both': 2200.0, 'o_:both': -500.0, 'sc:both': 700.0, 'px:heavy1': -1000.0, 'post1': -700.0, 'hm:post1': 1500.0, 'ya:pre0': -2800.0, 'yd:post1': 1100.0, 'os:post0': -1600.0, 'gg:heavy1': 2200.0, 'se:post1': 700.0, 'p1:post0': -400.0, 'xu:post1': 2800.0, 'hm:post0': 3600.0, 'tt:both': 1500.0}
+def place(o, s, c, free):
+    if o["kind"] == "arr":
+        return s + c["rem"]
+    free[o["eng"]] = s + cost(o, c)
+    if o["kind"] == "dma":
+        b = max(s + c["dma"] * 0.6, free.get("wire", 0.0))
+        free["wire"] = b + o["n"] / c["bw"]
+        return free["wire"] + c["dma"] * 0.4
+    return free[o["eng"]]
 
 
-def tune(o):
-    kind = o["name"][:2] + ":" + o["tag"]
-    return TUNE.get(o["tag"], 0.0) + TUNE.get(o["name"], 0.0) + TUNE.get(kind, 0.0)
+def justify(seq, before, dur, eng):
+    start, line = {None: 0.0}, {}
+    for i in seq:
+        s = max([start[j] + gap for j, gap in before[i]])
+        d = dur[i]
+        if d > 0:
+            taken = line.setdefault(eng[i], [])
+            k = len(taken)
+            while k > 0 and taken[k - 1][1] > s:
+                k -= 1
+            while k < len(taken) and taken[k][0] < s + d:
+                s = max(s, taken[k][1]); k += 1
+            taken.insert(k, (s, s + d))
+        start[i] = s
+    return start
 
 
-def schedule(ops, c):
-    sess = depend(ops)
+def replay(ops, order, c):
+    end, start, free = {}, {}, {}
+    for i in order:
+        start[i] = ready_at(ops, ops[i], end, free, c)
+        end[i] = place(ops[i], start[i], c, free)
+    return max(end.values()), start, end
+
+
+def schedule(ops, c, tries=None):
+    depend(ops)
     n = len(ops)
-    succ = [[] for _ in range(n)]
+    dur = [cost(o, c) for o in ops]
+    eng = [o["eng"] for o in ops]
+    kind = [o["name"][:2] + o["name"][4:5] for o in ops]
+    kinds = sorted(set(kind))
+    total, start, end = replay(ops, range(n), c)
+    extra = [end[i] - start[i] - dur[i] for i in range(n)]
+    fwd, bwd = [[(None, 0.0)] for _ in ops], [[] for _ in ops]
     for i, o in enumerate(ops):
         for j in o["dep"]:
-            succ[j].append(i)
-    prio = [0.0] * n
-    for i in range(n - 1, -1, -1):
-        own = finish(ops[i], 0.0, c, [0.0]) + c["lat"]
-        prio[i] = own + max([prio[j] for j in succ[i]] + [0.0])
-    for i in range(n):
-        prio[i] += tune(ops[i])
-    left = [len(o["dep"]) for o in ops]
-    ready = [i for i in range(n) if left[i] == 0]
-    end, free, order, holder, done = {}, {}, [], {}, set()
-    dmafree = [0.0]
-    while ready:
-        cand = []
-        for i in ready:
-            o = ops[i]; b = o["bank"]
-            extra = []
-            if b is not None and b[0] not in ORDERED and sess[b][0] == i and b[0] in holder:
-                extra = sess[holder[b[0]]]
-                if any(j not in done for j in extra):
-                    continue
-            keep = o["dep"]
-            o["dep"] = keep | set(extra)
-            cand.append((ready_at(ops, o, end, free, c), i, extra))
-            o["dep"] = keep
-        first = min(cand)
-        eng = ops[first[1]]["eng"]
-        s, i, extra = max((e for e in cand if ops[e[1]]["eng"] == eng and e[0] <= first[0] + TUNE["slack"]), key=lambda e: (prio[e[1]] - TUNE["lam"] * e[0], -e[1]))
-        o = ops[i]
-        o["dep"] = o["dep"] | set(extra)
-        if o["bank"] is not None:
-            holder[o["bank"][0]] = o["bank"]
-        end[i] = finish(o, s, c, dmafree)
-        if o["eng"] != "net":
-            free[o["eng"]] = s + cost(o, c)
-        o["t"] = (s, end[i])
-        order.append(i); done.add(i); ready.remove(i)
-        for j in succ[i]:
-            left[j] -= 1
-            if left[j] == 0:
-                ready.append(j)
-    assert len(order) == n
+            gap = 0.0 if j not in o["hard"] else extra[j] + (c["own"] if eng[i] == eng[j] else c["lat"])
+            fwd[i].append((j, dur[j] + gap)); bwd[j].append((i, dur[j] + gap))
+    dated = [(i, int(o["name"][2]), int(o["name"][4])) for i, o in enumerate(ops) if o["kind"] == "arr"]
+
+    def plan(period, lag, lead):
+        late = [STEPS * period + 2 * c["dma"] - dur[i] - extra[i] for i in range(n)]
+        for i, t, hf in dated:
+            late[i] = period * (t + lag * hf)
+        rank = [0.0] * n
+        for i in range(n - 1, -1, -1):
+            late[i] = min([late[i]] + [late[j] - gap for j, gap in bwd[i]])
+            rank[i] = min([late[i] - lead.get(kind[i], 0.0)] + [rank[j] - 1.0 for j, gap in bwd[i]])
+        early = justify(sorted(range(n), key=lambda i: rank[i]), fwd, dur, eng)
+        order = sorted(range(n), key=lambda i: (early[i], i))
+        return replay(ops, order, c)[0], order
+
+    best = min((plan(p, l, {})[0], p, l) for p in range(8000, 14000, 500) for l in (0.35, 0.45, 0.55))
+    total, period, lag = best
+    lead, seed = {}, 12345
+    for r in range(TRIES if tries is None else tries):
+        trial = dict(lead)
+        for e in range(2):
+            seed = (seed * 1103515245 + 12345) % 2147483648
+            k = kinds[(seed >> 8) % len(kinds)]
+            seed = (seed * 1103515245 + 12345) % 2147483648
+            trial[k] = trial.get(k, 0.0) + ((seed >> 8) % 4001 - 2000)
+        value = plan(period, lag, trial)[0]
+        if value <= total:
+            total, lead = value, trial
+    order = plan(period, lag, lead)[1]
+    total, start, end = replay(ops, order, c)
+    for i, o in enumerate(ops):
+        o["t"] = (start[i], end[i])
     return order
+
+
+TRIES = 2000
 
 
 def emit(g, T, ops, order):
@@ -466,18 +493,16 @@ def emit(g, T, ops, order):
     count = {"pe": 0, "dve": 0, "act": 0, "pool": 0}
     mark, seen, sent = {}, {e: {} for e in q}, 0
     needed = set()
-    for i in order:
-        for j in ops[i]["dep"]:
-            if not soft(ops[i], ops[j]):
-                needed.add(j)
+    for o in ops:
+        needed.update(o["hard"])
     for i in order:
         o = ops[i]; e = o["eng"]
         if e == "net":
             mark[i] = (o["name"], o["n"])
             continue
         want = {}
-        for j in o["dep"]:
-            if j in mark and not soft(o, ops[j]):
+        for j in o["hard"]:
+            if j in mark:
                 s, v = mark[j]
                 want[s] = max(want.get(s, 0), v)
         for s in sorted(want):
@@ -499,8 +524,15 @@ def emit(g, T, ops, order):
         g.wait_ge(T.sem[s], 16)
 
 
+ORDER = []
+
+
 def rank_program(g, core, T, topo):
     if T.rank_of(core) is None:
         return
     ops = build(g, T, topo, core)
-    emit(g, T, ops, schedule(ops, COST))
+    if not ORDER:
+        ORDER.extend(schedule(ops, COST))
+    else:
+        depend(ops)
+    emit(g, T, ops, ORDER)

@@ -28,7 +28,7 @@ SCRATCH = {
     "CC": (SB, [128, 16], "float32"), "CX": (SB, [128, 8], "float32"), "MC": (SB, [128, 24], "float32"),
     "RR": (SB, [128, 256], "bfloat16"), "AT": (SB, [128, 256], "uint16"),
     "YD": (SB, [128, 16, 16], "float16"), "YA": (SB, [128, 16, 16], "float16"), "YG": (SB, [128, 16, 16], "bfloat16"),
-    "SG": (SB, [128, 256], "bfloat16"), "FAR": (SB, [128, 256], "bfloat16"), "DZ": (SB, [128, 256], "float16"), "KS": (SB, [128, 128, 2], "float32"),
+    "SG": (SB, [128, 256], "bfloat16"), "FAR": (SB, [128, 256], "bfloat16"), "DZ": (SB, [128, 256], "float16"), "KS": (SB, [128, 128, 2], "int32"),
     "KI": (SB, [128, 16], "int32"), "LL": (SB, [128, 2, 5, 8], "int32"), "RQ": (SB, [128, 2, 5, 8], "bfloat16"), "LU": (SB, [128, 32], "uint16"),
     "SW": (SB, [128, 16], "float32"), "ZB": (SB, [128, 16], "int32"), "ZC": (SB, [128, 16], "int32"), "LS": (SB, [128, 16], "uint16"),
     "TT": (SB, [128, 16], "float32"), "HH": (SB, [128, 16], "bfloat16"),
@@ -230,8 +230,7 @@ def build(g, T, topo, core):
     def notes(u, hs, win, wk, a, ak):
         ts = slice(8 * hs[0], 8 * hs[-1] + 8); n = 8 * len(hs); f = ["%d" % hf for hf in hs]
         vts("zb" + u, T.ZB[:, ts], T.LL[:, hs[0]:hs[-1] + 1, 3, :], 0x1700, None, A.bitwise_and, None, ["Z" + e for e in f], ["ZB" + e for e in f], n)
-        vtt("zc" + u, T.ZC[:, ts], T.ZB[:, ts], T.CC[:, ts], A.add, ["ZB" + e for e in f] + ["CC"], ["ZC" + e for e in f], n)
-        vcp("ls" + u, T.LS[:, ts], T.ZC[:, ts], ["ZC" + e for e in f], ["LS" + e for e in f], n)
+        vtt("ls" + u, T.LS[:, ts], T.ZB[:, ts], T.CC[:, ts], A.add, ["ZB" + e for e in f] + ["CC"], ["LS" + e for e in f], n)
         vcp("sc" + u, win.indirect(T.LS[:, ts]), a, ["LS" + e for e in f] + ak, wk, 16 * n, kind="sca")
 
     def post(t, hf):
@@ -252,11 +251,11 @@ def build(g, T, topo, core):
                ["RS"], ["KS%d" % e + f], "el", 64, bk)
         km = T.KS[:, 64 * hf + 15:64 * hf + 64:16, :]
         L, Q = T.LL, T.RQ
-        vcp("ki" + u, T.KI[:, ts], km, ["KS0" + f, "KS1" + f], ["KI" + f], 8)
+        ks = ["KS0" + f, "KS1" + f]
         vts("ng" + u, Q[:, hf, 2, :], km, -16711680.0, 4096.0, A.is_ge, A.mult, ["KS0" + f, "KS1" + f], ["NG" + f], 8)
-        vts("kk" + u, L[:, hf, 1, :], T.KI[:, ts], 11, 15, A.logical_shift_right, A.bitwise_and, ["KI" + f], ["KK" + f], 8)
-        vts("nn" + u, L[:, hf, 0, :], T.KI[:, ts], 2047, None, A.bitwise_and, None, ["KI" + f], ["N" + f], 8)
-        vts("oo" + u, L[:, hf, 2, :], T.KI[:, ts], 11, 31, A.logical_shift_right, A.bitwise_and, ["KI" + f], ["OO" + f], 8)
+        vts("kk" + u, L[:, hf, 1, :], km, 11, 15, A.logical_shift_right, A.bitwise_and, ks, ["KK" + f], 8)
+        vts("nn" + u, L[:, hf, 0, :], km, 2047, None, A.bitwise_and, None, ks, ["N" + f], 8)
+        vts("oo" + u, L[:, hf, 2, :], km, 11, 31, A.logical_shift_right, A.bitwise_and, ks, ["OO" + f], 8)
         vtt("zx" + u, L[:, hf, 3:5, :], L[:, hf, 0:2, :], Q[:, hf, 2:4, :], A.add, ["N" + f, "KK" + f, "NG" + f, "CX" + f], ["Z" + f, "LP" + f], 16)
         vtt("lp" + u, L[:, hf, 4, :], L[:, hf, 4, :], L[:, hf, 3, :], A.min, ["LP" + f, "Z" + f], ["LP" + f], 8)
         lu = T.LU[:, 16 * hf:16 * hf + 16]
@@ -451,7 +450,33 @@ def schedule(ops, c, tries=None):
         for j in o["dep"]:
             gap = 0.0 if j not in o["hard"] else extra[j] + (c["own"] if eng[i] == eng[j] else c["lat"])
             fwd[i].append((j, dur[j] + gap)); bwd[j].append((i, dur[j] + gap))
+    last = {}
+    for i, o in enumerate(ops):
+        if o["name"][:5] in last and o["name"][3:4] == "_":
+            j = last[o["name"][:5]]
+            bwd[j].append((i, dur[j]))
+        last[o["name"][:5]] = i
     dated = [(i, int(o["name"][2]), int(o["name"][4])) for i, o in enumerate(ops) if o["kind"] == "arr"]
+
+    others = []
+    for v in VARIANTS:
+        m = dict(c); m.update(v)
+        others.append((m, [cost(o, m) for o in ops], [[(j, m["own"] if eng[i] == eng[j] else m["lat"]) for j in o["hard"]] for i, o in enumerate(ops)]))
+    plain = [o["kind"] not in ("dma", "arr") for o in ops]
+
+    def length(order, model):
+        m, d, hard = model
+        end, free = [0.0] * n, {e: 0.0 for e in eng}
+        for i in order:
+            s = free[eng[i]]
+            for j, gap in hard[i]:
+                if end[j] + gap > s:
+                    s = end[j] + gap
+            if plain[i]:
+                end[i] = free[eng[i]] = s + d[i]
+            else:
+                end[i] = place(ops[i], s, m, free)
+        return max(end)
 
     def plan(period, lag, lead):
         late = [STEPS * period + 2 * c["dma"] - dur[i] - extra[i] for i in range(n)]
@@ -463,29 +488,40 @@ def schedule(ops, c, tries=None):
             rank[i] = min([late[i] - lead.get(kind[i], 0.0)] + [rank[j] - 1.0 for j, gap in bwd[i]])
         early = justify(sorted(range(n), key=lambda i: rank[i]), fwd, dur, eng)
         order = sorted(range(n), key=lambda i: (early[i], i))
-        return replay(ops, order, c)[0], order
+        return sum(length(order, m) for m in others) / len(others), order
 
     best = min((plan(p, l, {})[0], p, l) for p in range(8000, 14000, 500) for l in (0.35, 0.45, 0.55))
     total, period, lag = best
-    lead, seed = {}, 12345
-    for r in range(TRIES if tries is None else tries):
-        trial = dict(lead)
-        for e in range(2):
-            seed = (seed * 1103515245 + 12345) % 2147483648
-            k = kinds[(seed >> 8) % len(kinds)]
-            seed = (seed * 1103515245 + 12345) % 2147483648
-            trial[k] = trial.get(k, 0.0) + ((seed >> 8) % 4001 - 2000)
-        value = plan(period, lag, trial)[0]
-        if value <= total:
-            total, lead = value, trial
-    order = plan(period, lag, lead)[1]
+    seed = [SEED]
+
+    def draw(m):
+        seed[0] = (seed[0] * 1103515245 + 12345) % 2147483648
+        return (seed[0] >> 8) % m
+    now, tries = (total, period, lag, {}), TRIES if tries is None else tries
+    best = now
+    for r in range(tries):
+        value, period, lag, lead = now
+        lead = dict(lead)
+        if draw(20) == 0:
+            period, lag = period + draw(401) - 200, lag + (draw(41) - 20) / 500.0
+        for e in range(1 + draw(2)):
+            k = kinds[draw(len(kinds))]
+            lead[k] = lead.get(k, 0.0) + (draw(4001) - 2000) * (1.0 if draw(2) else 0.2)
+        trial = plan(period, lag, lead)[0]
+        if trial <= value + SLACK * (1.0 - r / tries) * draw(100) / 100.0:
+            now = (trial, period, lag, lead)
+            if trial < best[0]:
+                best = now
+    order = plan(*best[1:])[1]
     total, start, end = replay(ops, order, c)
     for i, o in enumerate(ops):
         o["t"] = (start[i], end[i])
     return order
 
 
-TRIES = 2000
+TRIES, SEED, SLACK = 4000, 12345, 100.0
+VARIANTS = [{}, {"cyc": 0.83, "pe": 0.42, "fix": 0.0, "lat": 250.0, "own": 60.0, "rem": 1200.0},
+            {"cyc": 1.0, "pe": 0.5, "fix": 0.0, "lat": 100.0, "own": 30.0}, {"cyc": 0.83, "pe": 0.42, "fix": 60.0, "lat": 60.0, "own": 30.0, "rem": 1800.0}]
 
 
 def emit(g, T, ops, order):

from concourse.mybir import AluOpType as A, ActivationFunctionType as F

STEPS = 5
OPT = {
    "gat": [32, 32, 32, 32],
    "mx": [64, 32, 32],
    "pm": [64, 64],
    "rr": "act",
    "speech": "dve",
    "conv": 4,
}

SB = "sbuf"
SCRATCH = {
    "CU": (SB, [128, 4096], "bfloat16"), "XW0": (SB, [128, 4096], "bfloat16"), "XW1": (SB, [128, 4096], "bfloat16"),
    "MX0": (SB, [128, 2048], "bfloat16"), "MX1": (SB, [128, 2048], "bfloat16"),
    "TB": (SB, [128, 10240], "int32"), "GO": (SB, [128, 6144], "float32"),
    "AI": (SB, [128, 256], "int32"), "AH": (SB, [128, 512], "float16"), "YS": (SB, [128, 256], "float32"),
    "HL": (SB, [128, 1536], "bfloat16"), "SP": (SB, [128, 1280], "bfloat16"),
    "WT": (SB, [128, 8], "int32"), "WF": (SB, [128, 8], "float32"),
    "ONE": (SB, [128, 128], "bfloat16"), "IW": (SB, [128, 160], "bfloat16"), "BO": (SB, [128, 128], "bfloat16"), "BO1": (SB, [128, 128], "bfloat16"),
    "NI": (SB, [128, 128], "bfloat16"), "IDH": (SB, [128, 128], "float16"), "BM2": (SB, [128, 128], "bfloat16"), "I8": (SB, [128, 128], "bfloat16"),
    "E4": (SB, [128, 144], "bfloat16"), "EM2": (SB, [128, 144], "bfloat16"), "ET": (SB, [128, 2048], "bfloat16"),
    "WB": (SB, [128, 128], "bfloat16"), "OM": (SB, [128, 128], "bfloat16"),
    "SA": (SB, [128, 512], "float16"), "SS": (SB, [128, 512], "bfloat16"), "SD": (SB, [128, 512], "float16"),
    "CK": (SB, [128, 128], "bfloat16"), "RS": (SB, [128, 128], "float32"),
    "PI": (SB, [128, 8], "int32"), "COL": (SB, [128, 16], "float32"), "IR": (SB, [128, 128], "float32"), "LM": (SB, [128, 16], "float32"),
    "CC": (SB, [128, 16], "float32"), "CX": (SB, [128, 8], "float32"), "MC": (SB, [128, 24], "float32"),
    "RR": (SB, [128, 256], "bfloat16"), "AT": (SB, [128, 256], "uint16"),
    "YD": (SB, [128, 16, 16], "float16"), "YA": (SB, [128, 16, 16], "float16"), "YG": (SB, [128, 16, 16], "bfloat16"),
    "SG": (SB, [128, 256], "bfloat16"), "FAR": (SB, [128, 256], "bfloat16"), "DZ": (SB, [128, 256], "float16"), "KS": (SB, [128, 128, 2], "int32"),
    "KI": (SB, [128, 16], "int32"), "LL": (SB, [128, 2, 5, 8], "int32"), "RQ": (SB, [128, 2, 5, 8], "bfloat16"), "LU": (SB, [128, 32], "uint16"),
    "SW": (SB, [128, 16], "float32"), "ZB": (SB, [128, 16], "int32"), "ZC": (SB, [128, 16], "int32"), "LS": (SB, [128, 16], "uint16"),
    "TT": (SB, [128, 16], "float32"), "HH": (SB, [128, 16], "bfloat16"),
    "P1": (SB, [128, 256], "bfloat16"), "HM": (SB, [128, 256], "bfloat16"), "T1": (SB, [128, 256], "float32"), "XU": (SB, [128, 256], "bfloat16"),
    "H0": ("psum", [128, 128, 4], "float32"), "H1": ("psum", [128, 128, 4], "float32"),
    "P0": ("psum", [128, 512], "float32"), "P1b": ("psum", [128, 512], "float32"),
    "K0": ("psum", [128, 512], "float32"), "K1": ("psum", [128, 512], "float32"),
    "X2": ("psum", [128, 32, 16], "float32"),
}
DMAS = ["l_cu0", "l_cu1", "l_h", "l_a", "l_w", "l_t", "l_sp", "l_gap", "c_sw", "o_s0", "o_s1", "o_g", "o_h0", "o_h1"]
SEMAPHORES = ["pe", "dve", "act", "pool", "sent"] + DMAS + ["ar%d_%d" % (t, h) for t in range(STEPS) for h in range(2)]

COST = {"cyc": 0.9, "pe": 0.45, "gat": 1.56, "sca": 3.8, "fix": 30.0, "lat": 150.0, "own": 100.0, "dma": 2000.0, "bw": 250.0, "rem": 2500.0, "send": 300.0}


def cuts(sizes):
    out, s = [], 0
    for n in sizes:
        out.append((s, n)); s += n
    return out


def build(g, T, topo, core):
    rank = T.rank_of(core)
    ranks = len(T.cores)
    ops = []
    V, S, P = g.vector, g.scalar, g.tensor

    def op(name, eng, fn, r, w, kind, n, bank=None):
        ops.append({"name": name, "eng": eng, "fn": fn, "r": list(r), "w": list(w), "kind": kind, "n": n, "bank": bank, "stop": False})

    def vts(name, out, in0, s1, s2, o0, o1, r, w, n, bank=None):
        if o1 is None:
            op(name, "dve", lambda: V.tensor_scalar(out, in0, s1, None, o0), r, w, "el", n, bank)
        else:
            op(name, "dve", lambda: V.tensor_scalar(out, in0, s1, s2, o0, o1), r, w, "el", n, bank)

    def vtt(name, out, a, b, o, r, w, n, bank=None, kind="el"):
        op(name, "dve", lambda: V.tensor_tensor(out, a, b, o), r, w, kind, n, bank)

    def vcp(name, out, a, r, w, n, bank=None, kind="el"):
        op(name, "dve", lambda: V.tensor_copy(out, a), r, w, kind, n, bank)

    def vset(name, out, c, w, n):
        op(name, "dve", lambda: V.memset(out, c), [], w, "el", n)

    def vtr(name, out, a, r, w, n):
        op(name, "dve", lambda: V.transpose(out, a), r, w, "el", n)

    def act(name, out, a, f, r, w, n, bank=None, kind="el", **kw):
        op(name, "act", lambda: S.activation(out, a, f, **kw), r, w, kind, n, bank)

    def mm(name, lst, r, w, bank, piece=4):
        if len(lst) > piece:
            for j in range(0, len(lst), piece):
                mm(name + "." + str(j), lst[j:j + piece], r, w, bank, piece)
            return

        def fn():
            last = None
            for (o, l, x, st, sp, n) in lst:
                last = P.matmul(o, l, x, st, sp)
            return last
        op(name, "pe", fn, r, w, "pe", sum(max(64, e[5]) for e in lst), bank)
        ops[-1]["stop"] = lst[-1][4]

    def dma(name, q, out, a, r, w, nbytes):
        e = {"sync": g.sync, "act": g.scalar, "pool": g}[q]
        op(name, q, lambda: e.dma_start(out, a), r, w, "dma", nbytes)

    def pool(name, fn, r, w, n):
        op(name, "pool", fn, r, w, "pool", n)

    XW = [T.XW0, T.XW1]; MX = [T.MX0, T.MX1]; HB = [T.H0, T.H1]; PB = [T.P0, T.P1b]; KB = [T.K0, T.K1]
    ID = T.IW[:, 16:144]

    dma("l_w", "act", T.WT[:, 0:1], T.w[:], [], ["WTw"], 4096)
    dma("l_t", "act", T.WT[:, 4:5], T.th[:], [], ["WTt"], 4096)
    dma("l_h", "sync", T.HL[:, 0:256], T.heard[:], [], ["h0_0", "h0_1", "q0"], 65536)
    dma("l_a", "sync", T.AI[:], T.scroll[:], ["q0"], ["AI", "q1"], 131072)
    dma("l_cu1", "sync", T.CU[:, 2048:4096], T.cues[:, 0:2048], ["q1"], ["CUb", "q2"], 524288)
    dma("l_cu0", "sync", T.CU[:, 0:2048], T.cues[:, 2048:4096], ["q2"], ["CUa", "q3"], 524288)
    dma("l_sp", "sync", T.TB[:, 0:2048], T.spare[:], ["q3"], ["spare", "q4"], 1048576)

    vset("one", T.ONE[:], 1.0, ["ONE"], 64)
    vset("one2", T.IW[:], 1.0, ["IW"], 80)
    pool("pi", lambda: g.iota(T.PI[:, 0:1], [[0, 1]], 0, 1), [], ["PI0"], 1)
    pool("bo1", lambda: g.affine_select(T.BO1[:], T.ONE[:], [[-16, 8], [0, 16]], A.is_ge, 0.0, 0, 1), ["ONE"], ["BO1"], 128)
    pool("bo", lambda: g.affine_select(T.BO[:], T.BO1[:], [[16, 8], [0, 16]], A.is_ge, 0.0, 15, -1), ["BO1"], ["BO"], 128)
    pool("iw", lambda: g.affine_select(T.IW[:], T.IW[:], [[-1, 160]], A.is_equal, 0.0, 16, 1), ["IW"], ["IW"], 160)
    pool("ir", lambda: g.iota(T.IR[:], [[0, 8], [1, 16]], 0, 0, allow_small_or_imprecise_dtypes=True), [], ["IR"], 128)
    pool("cc", lambda: g.iota(T.CC[:], [[16, 16]], 0, 0, allow_small_or_imprecise_dtypes=True), [], ["CC"], 16)
    vts("lane", T.PI[:, 2:3], T.PI[:, 0:1], 15, None, A.bitwise_and, None, ["PI0"], ["PI2"], 1)
    vts("par", T.PI[:, 3:4], T.PI[:, 0:1], 4, 1, A.logical_shift_right, A.bitwise_and, ["PI0"], ["PI3"], 1)
    vcp("lanef", T.COL[:, 0:2], T.PI[:, 2:4], ["PI2", "PI3"], ["C01"], 2)
    LANE, ODD, EVEN = T.COL[:, 0:1], T.COL[:, 1:2], T.COL[:, 2:3]
    vts("even", EVEN, ODD, -1.0, 1.0, A.mult, A.add, ["C01"], ["C2"], 1)
    vts("dgc", T.COL[:, 3:4], LANE, 7.5, -4096.0, A.add, A.mult, ["C01"], ["C3"], 1)
    vts("sgb", T.COL[:, 4:5], LANE, -1.0, 0.5, A.mult, A.add, ["C01"], ["C4"], 1)
    vts("cc2", T.CC[:], T.CC[:], LANE, None, A.add, None, ["CC", "C01"], ["CC"], 16)
    for hf in range(2):
        vts("cx%d" % hf, T.RQ[:, hf, 3, :], T.CC[:, 0:8], 128.0, 16.0, A.add, A.mult, ["CC"], ["CX%d" % hf], 8)
    vcp("wf", T.WF[:, 0:1], T.WT[:, 0:1], ["WTw"], ["WFw"], 1)
    THR = T.MC[:, 20:21]
    vts("thr", THR, T.WT[:, 4:5], 2.0, None, A.mult, None, ["WTt"], ["THR"], 1)
    vts("tf", T.WF[:, 4:5], T.WT[:, 4:5], 7.5, 2.0, A.add, A.mult, ["WTt"], ["WFt"], 1)
    vts("wb", T.WB[:], T.BO[:], T.WF[:, 0:1], None, A.mult, None, ["BO", "WFw"], ["WB"], 64)
    vcp("idh", T.IDH[:], ID, ["IW"], ["IDH"], 64)
    for hf in range(2):
        vcp("a0%d" % hf, T.AH[:, 128 * hf:128 * hf + 128], T.AI[:, 128 * hf:128 * hf + 128], ["AI"], ["a0_%d" % hf], 128)
    act("ni", T.NI[:], ID, F.Identity, ["IW"], ["NI"], 128, scale=-1.0)
    vset("e4z", T.E4[:, 128:144], 0.0, ["E4z"], 8)
    vset("em2z", T.EM2[:, 128:144], 0.0, ["EM2z"], 8)
    vts("e1", T.BO1[:], T.IR[:], 15.0, None, A.is_equal, None, ["IR", "BO"], ["BO1"], 128)
    vtt("e2", T.BO1[:], T.BO1[:], T.BO[:], A.mult, ["BO1", "BO"], ["BO1"], 256)
    act("e4", T.E4[:, 0:128], T.BO1[:], F.Identity, ["BO1"], ["E4"], 128, scale=4.0)
    act("em2", T.EM2[:, 0:128], T.BO1[:], F.Identity, ["BO1"], ["EM2"], 128, scale=-2.0)
    act("i8", T.I8[:], ID, F.Identity, ["IW"], ["I8"], 128, scale=8.0)
    act("bm2", T.BM2[:], T.BO[:], F.Identity, ["BO"], ["BM2"], 128, scale=-2.0)
    vset("om", T.OM[:], -1.0 / 2048.0, ["OM"], 64)
    src = {0: (ID, EVEN), 1: (T.IW[:, 32:160], ODD), 2: (T.IW[:, 0:128], EVEN), 3: (ID, ODD)}
    for j in range(4):
        m, c = src[j]
        vts("sd%d" % j, T.SD[:, 128 * j:128 * j + 128], m, c, 32768.0, A.mult, A.mult, ["IW", "C01", "C2"], ["SD%d" % j], 64)
        vts("sa%d" % j, T.SA[:, 128 * j:128 * j + 128], m, c, None, A.mult, None, ["IW", "C01", "C2"], ["SA%d" % j], 64)
        vts("ss%d" % j, T.SS[:, 128 * j:128 * j + 128], m, c, 16384.0, A.mult, A.mult, ["IW", "C01", "C2"], ["SS%d" % j], 64)
    vts("lm", T.LM[:], T.IR[:, 0:16], LANE, -1.0, A.is_equal, A.mult, ["IR", "C01"], ["LM"], 16)
    for cl in range(16):
        if cl % 2:
            act("et%d" % cl, T.ET[:, 128 * cl:128 * cl + 128], T.BO[:], F.Identity, ["BO", "LM"], ["ET%d" % cl], 128, scale=T.LM[:, cl:cl + 1])
        else:
            vts("et%d" % cl, T.ET[:, 128 * cl:128 * cl + 128], T.BO[:], T.LM[:, cl:cl + 1], None, A.mult, None, ["BO", "LM"], ["ET%d" % cl], 64)
    ETK = ["ET%d" % cl for cl in range(16)]
    vset("ck0", T.CK[:], 0.0, ["CK"], 64)
    vts("ck1", T.CK[0:32, :], T.IR[0:32, :], 8.0, 64.0, A.add, A.mult, ["IR"], ["CK"], 128)
    vset("ck2", T.CK[32:64, :], -524288.0, ["CK"], 64)
    vts("rs", T.RS[:], T.IR[:], 0.0, 67108864.0, A.is_equal, A.mult, ["IR"], ["RS"], 128)
    vset("sg0", T.SG[:], -1.0, ["SG"], 128)
    vset("yg0", T.YG[:], -1.0, ["YG"], 128)
    vset("sw0", T.SW[:], 0.5, ["SW"], 16)
    vset("hh0", T.HH[:], -64.0, ["HH"], 16)
    pool("sw_e", lambda: g.affine_select(T.XW0[:, 0:2048:2], T.CU[:, 2049:4096:2], [[0, 1024]], A.is_gt, 0.0, 1, 0), ["CUb"], ["SWe"], 1024)
    pool("sw_o", lambda: g.affine_select(T.XW0[:, 1:2048:2], T.CU[:, 2048:4096:2], [[0, 1024]], A.is_gt, 0.0, 1, 0), ["CUb"], ["SWo"], 1024)
    dma("c_sw", "sync", T.XW1[:, 0:2048], T.XW0[:, 0:2048], ["SWe", "SWo", "q4"], ["SW1", "q5"], 524288)
    dma("l_gap", "sync", T.TB[:, 4096:6144], T.spare[:], ["q5"], ["gap"], 1048576)
    SWK = [["SWe", "SWo"], ["SW1"]]

    def turn(out, mats, y, hf, stop=False):
        return [(out[:, 64 * (j % 2):64 * (j % 2) + 64], mats[:, 128 * j:128 * j + 128], y[:, 8 * hf + j // 2:8 * hf + 8:2, :], False, stop and j == 3, 64) for j in range(4)]

    def state(t, hf):
        c0 = 128 * hf
        return (T.HL[:, 256 * t + c0:256 * t + c0 + 128], "h%d_%d" % (t, hf),
                T.AH[:, 256 * (t % 2) + c0:256 * (t % 2) + c0 + 128], "a%d_%d" % (t % 2, hf))

    def blocks(name, b0, n):
        return ["%s_%d" % (name, b) for b in range(b0 // 16, (b0 + n) // 16)]

    def pre(t, hf):
        c0 = 128 * hf; u = "%d_%d" % (t, hf); f = "%d" % hf
        h, hk, a, ak = state(t, hf)
        b1, b2, bh = ("K" + f, "v" + u), ("P" + f, "v" + u), ("H" + f, "h" + u)
        v1, v2 = KB[hf][:, 0:128], PB[hf][:, 0:128]
        mm("va" + u, [(v1, T.IDH[:], a, True, False, 128)], [ak, "IDH"], [], b1)
        mm("vb" + u, [(v2, T.IDH[:], a, True, False, 128)], [ak, "IDH"], [], b2)
        mm("v1" + u, [(v1, T.WB[:], h, False, True, 128)], [hk, "WB"], [], b1)
        mm("v2" + u, [(v2, T.WB[:], h, False, False, 128)], [hk, "WB"], [], b2)
        if OPT["rr"] == "act":
            act("rr" + u, T.RR[:, c0:c0 + 128], v1, F.Identity, [], ["RR" + f], 128, b1, bias=524288.5)
        else:
            vts("rr" + u, T.RR[:, c0:c0 + 128], v1, 524288.5, None, A.add, None, [], ["RR" + f], 128, b1)
        mm("v3" + u, [(v2, T.NI[:], T.RR[:, c0:c0 + 128], False, True, 128)], ["RR" + f, "NI"], [], b2)
        for e in range(2):
            vts("at" + u + "_%d" % e, T.AT[:, c0 + 64 * e:c0 + 64 * e + 64], PB[hf][:, 64 * e:64 * e + 64], 526336.0, None, A.add, None, [], blocks("AT" + f, 64 * e, 64), 64, b2)
        mm("h4" + u, [(HB[hf][:, :, r], ID, h, True, True, 128) for r in range(4)], [hk, "IW"], [], bh, 2)
        vtr("ya" + u, T.YA[:, 8 * hf:8 * hf + 8, :], a, [ak], ["YA" + f], 64)

    def heavy(t, hf):
        c0 = 128 * hf; u = "%d_%d" % (t, hf); f = "%d" % hf
        h, hk, a, ak = state(t, hf)
        X, M, D = XW[hf], MX[hf], PB[hf]
        bh, bp = ("H" + f, "h" + u), ("P" + f, "d" + u)
        mm("p0" + u, [(D[:, 0:128], T.BM2[:], h, True, False, 128)], ["BM2", hk], [], bp)
        for b0, n in cuts(OPT["gat"]):
            act("gg" + u + "_%d" % b0, X[:, 2048 + 16 * b0:2048 + 16 * (b0 + n)], T.CU[:].indirect(T.AT[:, c0 + b0:c0 + b0 + n]), F.Copy,
                ["CUa", "CUb"] + blocks("AT" + f, b0, n), blocks("x" + f, b0, n), 16 * n, kind="gat")
        for b0, n in cuts(OPT["pm"]):
            mm("px" + u + "_%d" % b0, [(D[:, b0:b0 + n], T.EM2[:, 15 - i:143 - i], X[:, 2048 + 16 * b0 + i:2048 + 16 * (b0 + n):16], False, False, n) for i in range(16)],
               blocks("x" + f, b0, n) + ["EM2", "EM2z"], [], bp)
        for b0, n in cuts(OPT["mx"]):
            for j in range(4):
                vtt("mx" + u + "_%d_%d" % (b0, j), M[:, 512 * j + 4 * b0:512 * j + 4 * (b0 + n)], X[:, 2048 + 16 * b0 + j:2048 + 16 * (b0 + n):4], HB[hf][:, b0:b0 + n, :], A.max,
                    blocks("x" + f, b0, n), blocks("m%d_%d" % (hf, j), b0, n), 4 * n, bh)
        for b0, n in cuts(OPT["pm"]):
            for j in range(4):
                mm("pm" + u + "_%d_%d" % (b0, j), [(D[:, b0:b0 + n], T.E4[:, 15 - i:143 - i], M[:, 512 * j + 4 * b0 + i // 4:512 * j + 4 * (b0 + n):4], False, b0 + n == 128 and i == 15, n) for i in range(j, 16, 4)],
                   blocks("m%d_%d" % (hf, j), b0, n) + ["E4", "E4z"], [], bp)

    def notes(u, hs, win, wk, a, ak):
        ts = slice(8 * hs[0], 8 * hs[-1] + 8); n = 8 * len(hs); f = ["%d" % hf for hf in hs]
        vts("zb" + u, T.ZB[:, ts], T.LL[:, hs[0]:hs[-1] + 1, 3, :], 0x1700, None, A.bitwise_and, None, ["Z" + e for e in f], ["ZB" + e for e in f], n)
        vtt("ls" + u, T.LS[:, ts], T.ZB[:, ts], T.CC[:, ts], A.add, ["ZB" + e for e in f] + ["CC"], ["LS" + e for e in f], n)
        vcp("sc" + u, win.indirect(T.LS[:, ts]), a, ["LS" + e for e in f] + ak, wk, 16 * n, kind="sca")

    def post(t, hf):
        c0 = 128 * hf; cs = slice(c0, c0 + 128); ts = slice(8 * hf, 8 * hf + 8)
        u = "%d_%d" % (t, hf); f = "%d" % hf
        h, hk, a, ak = state(t, hf)
        bp, bk, br, bs, bq = ("P" + f, "d" + u), ("K" + f, "k" + u), ("P" + f, "r" + u), ("K" + f, "s" + u), ("H" + f, "q" + u)
        D, K, R = PB[hf][:, 0:128], KB[hf][:, 0:128], PB[hf]
        mm("o0" + u, [(K, T.ONE[:], T.CK[:], True, False, 128)], ["ONE", "CK"], [], bk)
        mm("o1" + u, turn(KB[hf], T.SA, T.YA, hf), ["YA" + f, "SA0", "SA1", "SA2", "SA3"], [], bk)
        mm("o2" + u, turn(KB[hf], T.SS, T.YG, hf), ["YG", "SS0", "SS1", "SS2", "SS3"], [], bk)
        vts("far" + u, T.FAR[:, cs], D, THR, 1024.0, A.is_gt, A.mult, ["THR"], ["FAR" + f], 128, bp)
        vtt("dz" + u, T.DZ[:, cs], D, T.FAR[:, cs], A.min, ["FAR" + f], ["DZ" + f], 128, bp)
        vtr("yd" + u, T.YD[:, ts, :], T.DZ[:, cs], ["DZ" + f], ["YD" + f], 64)
        mm("k1" + u, turn(KB[hf], T.SD, T.YD, hf, True), ["YD" + f, "SD0", "SD1", "SD2", "SD3"], [], bk)
        for e in range(2):
            op("scan" + u + "_%d" % e, "dve", lambda e=e: V.tensor_tensor_scan(T.KS[:, 64 * hf:64 * hf + 64, e], T.RS[:, 0:64], KB[hf][:, 64 * e:64 * e + 64], 0.0, A.add, A.min),
               ["RS"], ["KS%d" % e + f], "el", 64, bk)
        km = T.KS[:, 64 * hf + 15:64 * hf + 64:16, :]
        L, Q = T.LL, T.RQ
        ks = ["KS0" + f, "KS1" + f]
        vts("ng" + u, Q[:, hf, 2, :], km, -16711680.0, 4096.0, A.is_ge, A.mult, ["KS0" + f, "KS1" + f], ["NG" + f], 8)
        vts("kk" + u, L[:, hf, 1, :], km, 11, 15, A.logical_shift_right, A.bitwise_and, ks, ["KK" + f], 8)
        vts("nn" + u, L[:, hf, 0, :], km, 2047, None, A.bitwise_and, None, ks, ["N" + f], 8)
        vts("oo" + u, L[:, hf, 2, :], km, 11, 31, A.logical_shift_right, A.bitwise_and, ks, ["OO" + f], 8)
        vtt("zx" + u, L[:, hf, 3:5, :], L[:, hf, 0:2, :], Q[:, hf, 2:4, :], A.add, ["N" + f, "KK" + f, "NG" + f, "CX" + f], ["Z" + f, "LP" + f], 16)
        vtt("lp" + u, L[:, hf, 4, :], L[:, hf, 4, :], L[:, hf, 3, :], A.min, ["LP" + f, "Z" + f], ["LP" + f], 8)
        lu = T.LU[:, 16 * hf:16 * hf + 16]
        lt_, lsp = T.LU[:, 16 * hf:16 * hf + 8], T.LU[:, 16 * hf + 8:16 * hf + 16]
        if t == 0:
            vcp("lu" + u, lu, L[:, hf, 0:5:4, :], ["N" + f, "LP" + f], ["LU" + f], 16)
            win, wk = T.TB[:, 0:2048], ["spare"]
        else:
            vcp("lu" + u, lu, L[:, hf, 3:5, :], ["Z" + f, "LP" + f], ["LU" + f], 16)
            win, wk = T.TB[:, 0:6144], ["spare", "gap"]
        vtt("ee" + u, Q[:, hf, 4, :], Q[:, hf, 2, :], T.SW[:, ts], A.mult, ["NG" + f, "SW"], ["EE" + f], 8)
        vtt("ju" + u, Q[:, hf, 0:2, :], L[:, hf, 1:3, :], Q[:, hf, 2:5:2, :], A.subtract, ["KK" + f, "OO" + f, "NG" + f, "EE" + f], ["J" + f, "U" + f], 16)
        mm("r0" + u, [(R[:, 0:128], T.I8[:], T.SG[:, cs], True, False, 128)], ["I8", "SG"], [], br)
        mm("r1" + u, [(R[:, cl:128:16], T.ET[:, 128 * cl:128 * cl + 128], Q[:, hf, 1, :], False, cl == 15, 8) for cl in range(16)], ETK + ["U" + f], [], br)
        bm = ("H" + f, "m" + u); hp = HB[hf][:, 32:64, :]
        mm("h0" + u, [(hp, ID, h, True, False, 128)], ["IW", hk], [], bm)
        mm("h1" + u, [(hp, T.BO[:], T.FAR[:, cs], False, True, 128)], ["BO", "FAR" + f], [], bm)
        act("hm" + u, T.HM[:, cs], hp, F.Relu, [], ["HM" + f], 128, bm, bias=-16384.0)
        act("p1" + u, T.P1[:, cs], R[:, 0:128], F.Relu, ["C3"], ["P1" + f], 128, br, scale=-4096.0, bias=T.COL[:, 3:4])
        sp = T.SP[:, 256 * t + c0:256 * t + c0 + 128]
        xk = SWK[hf] + blocks("x" + f, 0, 128) + ["LU" + f]
        if OPT["speech"] == "dve":
            vtt("xu" + u, T.XU[:, cs], XW[hf][:].indirect(lsp), T.HM[:, cs], A.subtract, xk + ["HM" + f], ["XU" + f], 128, kind="gat")
            act("sp" + u, sp, T.XU[:, cs], F.Abs, ["XU" + f], ["sp" + u], 128)
        else:
            act("xu" + u, T.XU[:, cs], XW[hf][:].indirect(lsp), F.Copy, xk, ["XU" + f], 128, kind="gat")
            mm("s" + u, [(K, ID, T.XU[:, cs], True, False, 128), (K, T.NI[:], T.HM[:, cs], False, True, 128)], ["XU" + f, "HM" + f, "IW", "NI"], [], bs)
            act("sp" + u, sp, K, F.Abs, [], ["sp" + u], 128, bs)
        dst = T.cores[(rank + 1 + t % (ranks - 1)) % ranks]
        rid, pid, _ = topo.addr(dst); mask = topo.mask(core, dst); ne = len(topo.engines(core, dst))
        land = T.HL[:, 256 * (t + 1) + c0:256 * (t + 1) + c0 + 128]
        op("send" + u, "pool", lambda: g.remote_dma(land, sp, T.sem["ar" + u], T.sem.sent, pid, rid, mask), ["sp" + u], ["snd" + u], "send", ne)
        op("ar" + u, "net", None, ["snd" + u], ["h%d_%d" % (t + 1, hf)], "arr", ne)
        vtt("t1" + u, T.T1[:, cs], win.indirect(lt_), T.P1[:, cs], A.min, wk + ["LU" + f, "P1" + f], ["T1" + f], 128, kind="gat")
        q = HB[hf][:, 0:32, :]
        mm("q" + u, [(q, T.IDH[:], a, True, False, 128), (q, T.NI[:], T.P1[:, cs], False, True, 128)], [ak, "IDH", "NI", "P1" + f], [], bq)
        if t < STEPS - 1:
            _, _, na, nk = state(t + 1, hf)
            vtt("an" + u, na, T.T1[:, cs], q, A.max, ["T1" + f], [nk], 128, bq)
        else:
            vtt("an" + u, T.YS[:, cs], T.T1[:, cs], q, A.max, ["T1" + f], ["YS" + f], 128, bq)
            dma("o_s" + f, "sync", T.ys[:, cs], T.YS[:, cs], ["YS" + f], ["ys" + f], 65536)
            dma("o_h" + f, "sync", T.yh[:, cs], land, ["h%d_%d" % (t + 1, hf)], ["yh" + f], 32768)
            notes(u, [hf], T.GO[:], ["go%d" % j for j in range(OPT["conv"])], a, [ak])

    def both(t):
        u = "%d" % t
        if t == STEPS - 1:
            dma("o_g", "act", T.yg[:], T.GO[:, 0:2048], ["go%d" % j for j in range(OPT["conv"])], ["yg"], 1048576)
            return
        notes(u, [0, 1], T.TB[:, 4096:10240], ["gap"], T.AH[:, 256 * (t % 2):256 * (t % 2) + 256], ["a%d_0" % (t % 2), "a%d_1" % (t % 2)])
        if t == STEPS - 2:
            n = 2048 // OPT["conv"]
            for j in range(OPT["conv"]):
                pool("cv%d" % j, lambda j=j: g.affine_select(T.GO[:, n * j:n * j + n], T.TB[:, 4096 + n * j:4096 + n * j + n], [[0, n]], A.is_gt, 0.0, 1, 0), ["gap"], ["go%d" % j], n)
        NG, EE = T.RQ[:, :, 2, :], T.RQ[:, :, 4, :]
        bm = ("X2", "m" + u); bh = ("X2", "h" + u)
        mm("mc" + u, [(T.X2[:, 0, :], T.OM[:], NG, True, True, 16)], ["OM", "NG0", "NG1"], [], bm)
        act("ma" + u, T.MC[:, 0:16], T.X2[:, 0, :], F.Identity, [], ["MC"], 200, bm, bias=255.0625, accum_out=T.MC[:, 16:17])
        vts("mr" + u, T.MC[:, 17:18], T.MC[:, 16:17], 402653184.0, 402653184.0, A.add, A.subtract, ["MC"], ["MR"], 1)
        vts("thr" + u, THR, T.MC[:, 16:17], T.MC[:, 17:18], T.WF[:, 4:5], A.subtract, A.add, ["WFt", "MC", "MR"], ["THR"], 1)
        vts("sw" + u, T.SW[:], EE, 1.0, 0.5, A.is_le, A.subtract, ["EE0", "EE1"], ["SW"], 16)
        vtt("tt" + u, T.TT[:], T.HH[:], EE, A.min, ["HH", "EE0", "EE1"], ["TT"], 16)
        vtt("hh" + u, T.HH[:], T.RQ[:, :, 0, :], T.TT[:], A.max, ["J0", "J1", "TT"], ["HH"], 16)
        mm("hr" + u, [(T.X2[:, 0:16, cl], T.ET[:, 128 * cl:128 * cl + 128], T.HH[:], True, True, 16) for cl in range(16)], ETK + ["HH"], [], bh)
        act("sg" + u, T.SG[:], T.X2[:, 0:16, :], F.Sign, ["C4"], ["SG"], 256, bh, scale=-1.0, bias=T.COL[:, 4:5])
        vtr("yg" + u, T.YG[:], T.SG[:], ["SG"], ["YG"], 128)

    for t in range(STEPS):
        for part in (pre, heavy, post):
            for hf in range(2):
                part(t, hf)
        both(t)
    return ops


def cost(o, c):
    k, n = o["kind"], o["n"]
    if k == "pe":
        return 10.0 + n * c["pe"]
    if k == "el":
        return c["fix"] + max(n, 64) * c["cyc"]
    if k == "gat":
        return 60.0 + n * c["gat"] * c["cyc"]
    if k == "sca":
        return 60.0 + n * c["sca"] * c["cyc"]
    if k == "pool":
        return 170.0 + 2 * n * c["cyc"]
    if k == "dma":
        return 60.0
    if k == "send":
        return c["send"]
    return 0.0


def depend(ops):
    writer, readers, sess, lastof = {}, {}, {}, {}
    for i, o in enumerate(ops):
        d = set()
        for k in o["r"]:
            if k in writer:
                d.add(writer[k])
        for k in o["w"]:
            if k in writer:
                d.add(writer[k])
            d.update(readers.get(k, []))
        for k in o["r"]:
            readers.setdefault(k, []).append(i)
        for k in o["w"]:
            writer[k] = i
            readers[k] = []
        b = o["bank"]
        if b is not None:
            if b in sess:
                d.update(j for j in sess[b] if j == sess[b][0] or o["stop"] or ops[j]["eng"] != o["eng"])
            elif b[0] in lastof:
                d.update(sess[lastof[b[0]]])
            sess.setdefault(b, []).append(i)
            lastof[b[0]] = b
        d.discard(i)
        o["dep"] = d
        o["hard"] = [j for j in d if not soft(o, ops[j])]


def soft(o, p):
    if o["eng"] != p["eng"]:
        return False
    if o["eng"] == "pe":
        return True
    shared = (set(o["r"]) & set(p["w"])) | (set(o["w"]) & set(p["r"])) | (set(o["w"]) & set(p["w"]))
    if o["kind"] == "dma" and p["kind"] == "dma":
        return all(k[0] == "q" for k in shared)
    if o["bank"] is not None and p["bank"] is not None and o["bank"][0] == p["bank"][0]:
        return not shared
    return False


def ready_at(ops, o, end, free, c):
    s = free.get(o["eng"], 0.0)
    for j in o["hard"]:
        s = max(s, end[j] + (c["own"] if ops[j]["eng"] == o["eng"] else c["lat"]))
    return s


def place(o, s, c, free):
    if o["kind"] == "arr":
        return s + c["rem"]
    free[o["eng"]] = s + cost(o, c)
    if o["kind"] == "dma":
        b = max(s + c["dma"] * 0.6, free.get("wire", 0.0))
        free["wire"] = b + o["n"] / c["bw"]
        return free["wire"] + c["dma"] * 0.4
    return free[o["eng"]]


def justify(seq, before, dur, eng):
    start, line = {None: 0.0}, {}
    for i in seq:
        s = max([start[j] + gap for j, gap in before[i]])
        d = dur[i]
        if d > 0:
            taken = line.setdefault(eng[i], [])
            k = len(taken)
            while k > 0 and taken[k - 1][1] > s:
                k -= 1
            while k < len(taken) and taken[k][0] < s + d:
                s = max(s, taken[k][1]); k += 1
            taken.insert(k, (s, s + d))
        start[i] = s
    return start


def replay(ops, order, c):
    end, start, free = {}, {}, {}
    for i in order:
        start[i] = ready_at(ops, ops[i], end, free, c)
        end[i] = place(ops[i], start[i], c, free)
    return max(end.values()), start, end


def schedule(ops, c, tries=None):
    depend(ops)
    n = len(ops)
    dur = [cost(o, c) for o in ops]
    eng = [o["eng"] for o in ops]
    kind = [o["name"][:2] + o["name"][4:5] for o in ops]
    kinds = sorted(set(kind))
    total, start, end = replay(ops, range(n), c)
    extra = [end[i] - start[i] - dur[i] for i in range(n)]
    fwd, bwd = [[(None, 0.0)] for _ in ops], [[] for _ in ops]
    for i, o in enumerate(ops):
        for j in o["dep"]:
            gap = 0.0 if j not in o["hard"] else extra[j] + (c["own"] if eng[i] == eng[j] else c["lat"])
            fwd[i].append((j, dur[j] + gap)); bwd[j].append((i, dur[j] + gap))
    last = {}
    for i, o in enumerate(ops):
        if o["name"][:5] in last and o["name"][3:4] == "_":
            j = last[o["name"][:5]]
            bwd[j].append((i, dur[j]))
        last[o["name"][:5]] = i
    dated = [(i, int(o["name"][2]), int(o["name"][4])) for i, o in enumerate(ops) if o["kind"] == "arr"]

    others = []
    for v in VARIANTS:
        m = dict(c); m.update(v)
        others.append((m, [cost(o, m) for o in ops], [[(j, m["own"] if eng[i] == eng[j] else m["lat"]) for j in o["hard"]] for i, o in enumerate(ops)]))
    plain = [o["kind"] not in ("dma", "arr") for o in ops]

    def length(order, model):
        m, d, hard = model
        end, free = [0.0] * n, {e: 0.0 for e in eng}
        for i in order:
            s = free[eng[i]]
            for j, gap in hard[i]:
                if end[j] + gap > s:
                    s = end[j] + gap
            if plain[i]:
                end[i] = free[eng[i]] = s + d[i]
            else:
                end[i] = place(ops[i], s, m, free)
        return max(end)

    def plan(period, lag, lead):
        late = [STEPS * period + 2 * c["dma"] - dur[i] - extra[i] for i in range(n)]
        for i, t, hf in dated:
            late[i] = period * (t + lag * hf)
        rank = [0.0] * n
        for i in range(n - 1, -1, -1):
            late[i] = min([late[i]] + [late[j] - gap for j, gap in bwd[i]])
            rank[i] = min([late[i] - lead.get(kind[i], 0.0)] + [rank[j] - 1.0 for j, gap in bwd[i]])
        early = justify(sorted(range(n), key=lambda i: rank[i]), fwd, dur, eng)
        order = sorted(range(n), key=lambda i: (early[i], i))
        return sum(length(order, m) for m in others) / len(others), order

    best = min((plan(p, l, {})[0], p, l) for p in range(8000, 14000, 500) for l in (0.35, 0.45, 0.55))
    total, period, lag = best
    seed = [SEED]

    def draw(m):
        seed[0] = (seed[0] * 1103515245 + 12345) % 2147483648
        return (seed[0] >> 8) % m
    now, tries = (total, period, lag, {}), TRIES if tries is None else tries
    best = now
    for r in range(tries):
        value, period, lag, lead = now
        lead = dict(lead)
        if draw(20) == 0:
            period, lag = period + draw(401) - 200, lag + (draw(41) - 20) / 500.0
        for e in range(1 + draw(2)):
            k = kinds[draw(len(kinds))]
            lead[k] = lead.get(k, 0.0) + (draw(4001) - 2000) * (1.0 if draw(2) else 0.2)
        trial = plan(period, lag, lead)[0]
        if trial <= value + SLACK * (1.0 - r / tries) * draw(100) / 100.0:
            now = (trial, period, lag, lead)
            if trial < best[0]:
                best = now
    order = plan(*best[1:])[1]
    total, start, end = replay(ops, order, c)
    for i, o in enumerate(ops):
        o["t"] = (start[i], end[i])
    return order


TRIES, SEED, SLACK = 4000, 12345, 100.0
VARIANTS = [{}, {"cyc": 0.83, "pe": 0.42, "fix": 0.0, "lat": 250.0, "own": 60.0, "rem": 1200.0},
            {"cyc": 1.0, "pe": 0.5, "fix": 0.0, "lat": 100.0, "own": 30.0}, {"cyc": 0.83, "pe": 0.42, "fix": 60.0, "lat": 60.0, "own": 30.0, "rem": 1800.0}]


def emit(g, T, ops, order):
    q = {"pe": g.tensor, "dve": g.vector, "act": g.scalar, "pool": g, "sync": g.sync}
    count = {"pe": 0, "dve": 0, "act": 0, "pool": 0}
    mark, seen, sent = {}, {e: {} for e in q}, 0
    needed = set()
    for o in ops:
        needed.update(o["hard"])
    for i in order:
        o = ops[i]; e = o["eng"]
        if e == "net":
            mark[i] = (o["name"], o["n"])
            continue
        want = {}
        for j in o["hard"]:
            if j in mark:
                s, v = mark[j]
                want[s] = max(want.get(s, 0), v)
        for s in sorted(want):
            if seen[e].get(s, 0) < want[s]:
                q[e].wait_ge(T.sem[s], want[s])
                seen[e][s] = want[s]
        ins = o["fn"]()
        if o["kind"] == "dma":
            ins.then_inc(T.sem[o["name"]], 16)
            mark[i] = (o["name"], 16)
        elif o["kind"] == "send":
            sent += o["n"]
        elif i in needed:
            count[e] += 1
            ins.then_inc(T.sem[e], 1)
            mark[i] = (e, count[e])
    g.wait_ge(T.sem.sent, sent)
    for s in ["o_s0", "o_s1", "o_h0", "o_h1", "o_g"]:
        g.wait_ge(T.sem[s], 16)


ORDER = []


def rank_program(g, core, T, topo):
    if T.rank_of(core) is None:
        return
    ops = build(g, T, topo, core)
    if not ORDER:
        ORDER.extend(schedule(ops, COST))
    else:
        depend(ops)
    emit(g, T, ops, ORDER)
